import numpy as np
import ml_dtypes


def mxq(x, axis, fmt="e4m3"):
    dtype, down = {"e4m3": (ml_dtypes.float8_e4m3fn, 7), "e5m2": (ml_dtypes.float8_e5m2, 14)}[fmt]
    v = np.moveaxis(np.asarray(x, np.float32).astype(ml_dtypes.bfloat16).astype(np.float64), axis, -1)
    blocks = v.reshape(v.shape[:-1] + (-1, 32))
    amax = np.abs(blocks).max(-1, keepdims=True)
    byte = np.maximum(np.where(amax > 0, np.frexp(amax)[1] - 1 + 127, 0) - down, 1)
    scale = np.exp2(byte - 127.0)
    codes = (blocks / scale).astype(np.float32).astype(dtype).astype(np.float64)
    return np.moveaxis((codes * scale).reshape(v.shape), -1, axis)


WIDE = False


def mx_kscale(k):
    if not WIDE:
        return np.ones(k)
    levels = np.array([10, -10, 5, -5, 0])
    if k % 512:
        return np.exp2(np.random.permutation(np.resize(levels, k // 32))).repeat(32)
    a = np.empty((k // 512, 16))
    for p in range(k // 512):
        a[p, :8] = np.random.permutation(np.resize(levels, 8))
        for g in range(8):
            far = levels[np.abs(levels - a[p, g]) >= 10]
            a[p, g + 8] = far[np.random.randint(len(far))]
    return np.exp2(a.ravel()).repeat(32)


def f64(x):
    return np.asarray(x).astype(np.float64)


def striped(idx):
    return np.tile(idx.reshape(-1, 16).T, (8, 1)).astype(np.uint16)


def unstriped(offs):
    return offs[:16].T.reshape(-1).astype(np.int64)


E2M1 = np.array([0.0, 0.5, 1.0, 1.5, 2.0, 3.0, 4.0, 6.0, -0.0, -0.5, -1.0, -1.5, -2.0, -3.0, -4.0, -6.0])


def pack_weight(w, fmt):
    k, n = w.shape
    w = f64(np.asarray(w, np.float32).astype(ml_dtypes.bfloat16)).reshape(k // 32, 32, n)
    amax = np.abs(w).max(1)
    if fmt == "e4m3":
        byte = np.frexp(amax)[1] - 1 + 127 - 7
    else:
        mant, ex = np.frexp(amax / 6.0)
        byte = np.where(mant > 0.5, ex, ex - 1) + 127
    byte = np.clip(np.where(amax > 0, byte, 1), 1, 254)
    scaled = (w * np.exp2(127.0 - byte)[:, None, :]).reshape(k, n).astype(np.float32)
    by_word = np.ascontiguousarray(scaled.reshape(k // 512, 128, 4, n).transpose(0, 1, 3, 2))
    if fmt == "e4m3":
        words = by_word.astype(ml_dtypes.float8_e4m3fn).view(np.uint8)
    else:
        c = by_word.astype(ml_dtypes.float4_e2m1fn).view(np.uint8) & 0xF
        words = (c[..., 0::2] | (c[..., 1::2] << 4)).reshape(k // 512, 128, 2 * n)
    return np.ascontiguousarray(words), np.ascontiguousarray(byte.astype(np.uint8).reshape(k // 512, 16, n))


def unpack_weight(words, scales, fmt):
    g, _, n = scales.shape
    words = np.ascontiguousarray(words).reshape(g, 128, n, -1)
    if fmt == "e4m3":
        vals = words.view(ml_dtypes.float8_e4m3fn).astype(np.float64)
    else:
        nib = np.empty((g, 128, n, 4), np.uint8)
        nib[..., 0::2] = words & 0xF
        nib[..., 1::2] = words >> 4
        vals = E2M1[nib]
    vals = vals * np.repeat(np.exp2(scales.astype(np.float64) - 127.0), 8, axis=1)[..., None]
    return vals.transpose(0, 1, 3, 2).reshape(g * 512, n)


def relu(v):
    return np.maximum(v, 0.0)


K, T, E, C, H, N = 512, 768, 12, 128, 512, 512


def by_expert(wq, xq):
    return np.concatenate([wq[e].T @ xq[:, e * C:(e + 1) * C] for e in range(E)], axis=1)


def setup_inputs():
    n = np.random.standard_normal
    s = mx_kscale(K)
    u = mx_kscale(H)
    first = np.random.permutation(np.repeat(np.arange(E), T // E))
    second = (first + 1 + np.random.permutation(np.repeat(np.arange(E - 1), -(-T // (E - 1)))[:T])) % E
    while np.bincount(second, minlength=E).max() != T // E:
        load = np.bincount(second, minlength=E); hi, lo = int(load.argmax()), int(load.argmin())
        t = np.flatnonzero((second == hi) & (first != lo))[0]; second[t] = lo
    slot_token = np.empty(E * C, np.int64); pos = np.empty((2, T), np.int64); fill = np.zeros(E, np.int64)
    place = np.stack([np.random.permutation(C) for _ in range(E)])
    for r, deal in enumerate((first, second)):
        for t in np.random.permutation(T):
            e = deal[t]; j = e * C + place[e, fill[e]]; fill[e] += 1; slot_token[j] = t; pos[r, t] = j
    g = np.random.uniform(0.2, 0.8, T)
    x = pack_weight(n((K, T)) * s[:, None], "e4m3")
    w = [pack_weight(m, "e2m1") for m in n((E, K, N)) / np.sqrt(K) / s[None, :, None]]
    wa = [pack_weight(m, "e4m3") for m in n((E, K, H)) / np.sqrt(K) / s[None, :, None] * u]
    wb = [pack_weight(m, "e4m3") for m in n((E, H, N)) / np.sqrt(H) / u[None, :, None]]
    return {
        "x_words": x[0],
        "x_scales": x[1],
        "w_words": np.stack([m[0] for m in w]),
        "w_scales": np.stack([m[1] for m in w]),
        "wa_words": np.stack([m[0] for m in wa]),
        "wa_scales": np.stack([m[1] for m in wa]),
        "wb_words": np.stack([m[0] for m in wb]),
        "wb_scales": np.stack([m[1] for m in wb]),
        "gate": np.stack([np.tile(g, (128, 1)), np.tile(1.0 - g, (128, 1))]).astype(np.float32),
        "offs": striped(slot_token),
        "pos1": striped(pos[0]),
        "pos2": striped(pos[1]),
    }


def reference(x_words, x_scales, w_words, w_scales, wa_words, wa_scales, wb_words, wb_scales, gate, offs, pos1, pos2):
    w = np.stack([unpack_weight(w_words[e], w_scales[e], "e2m1") for e in range(E)])
    wa = np.stack([unpack_weight(wa_words[e], wa_scales[e], "e4m3") for e in range(E)])
    wb = np.stack([unpack_weight(wb_words[e], wb_scales[e], "e4m3") for e in range(E)])
    idx = unstriped(offs)
    xq = unpack_weight(x_words, x_scales, "e4m3")[:, idx]
    h = relu(by_expert(wa, xq))
    y = by_expert(w, xq) + by_expert(wb, mxq(h, 0, "e4m3"))
    out = sum(f64(gate[r, :1]) * y[:, unstriped(p)] for r, p in enumerate((pos1, pos2)))
    return out

@@ -1,0 +1,214 @@
+from contextlib import ExitStack
+
+import concourse.mybir as mybir
+from concourse.masks import make_identity
+
+K, T, E, C, H, N = 512, 768, 12, 128, 512, 512
+S = E * C
+P = 128
+FLOPS = 2 * 3 * S * K * N
+
+F32 = mybir.dt.float32
+BF16 = mybir.dt.bfloat16
+I32 = mybir.dt.int32
+U32 = mybir.dt.uint32
+U16 = mybir.dt.uint16
+U8 = mybir.dt.uint8
+FP8X4 = mybir.dt.float8_e4m3fn_x4
+FP4X4 = mybir.dt.float4_e2m1fn_x4
+ACT = mybir.ActivationFunctionType
+MULT = mybir.AluOpType.mult
+ADD = mybir.AluOpType.add
+
+NT = N // P
+PAIRS = E // 2
+WA_ROW = 4
+WB_ROW = 8
+SCALAR_PAIRS = (3, 4, 5)
+LAST_CUTS = (0, 512, 768)
+WA_CUTS = (0, 2, 5, 8, 10, 12)
+
+
+def tile_moe_elr_relu_kernel(
+    tc, x_words, x_scales, w_words, w_scales, wa_words, wa_scales, wb_words, wb_scales, gate, offs, pos1, pos2, out
+):
+    nc = tc.nc
+    with ExitStack() as ctx:
+        lists = ctx.enter_context(tc.tile_pool(name="lists", bufs=1))
+        keep = ctx.enter_context(tc.tile_pool(name="keep", bufs=1))
+        ring = ctx.enter_context(tc.tile_pool(name="ring", bufs=3))
+        psum = ctx.enter_context(tc.psum_pool(name="psum", bufs=1))
+
+        offs_t = lists.tile([P, S // 16], U16, name="offs_t")
+        pos_t = [lists.tile([P, T // 16], U16, name="pos%d_t" % r) for r in (1, 2)]
+
+        xw = keep.tile([P, T], I32, name="xw", align_bytes=64)
+        xs = keep.tile([P, T], U8, name="xs", align_bytes=64)
+        wa_sc = keep.tile([P, E, H], U8, name="wa_sc", align_bytes=64)
+        wy_sc = keep.tile([P, E, N], U8, name="wy_sc", align_bytes=64)
+        chunks = list(zip(WA_CUTS[:-1], WA_CUTS[1:]))
+        wa_t = [keep.tile([P, b - a, H], I32, name="wa_t%d" % a, align_bytes=64) for a, b in chunks]
+        wb_t = [keep.tile([P, E, P], I32, name="wb_t%d" % j, align_bytes=64) for j in range(NT)]
+        w_t = [keep.tile([P, E, 2 * P], U8, name="w_t%d" % j, align_bytes=64) for j in range(NT)]
+        gate_t = [keep.tile([P, T], F32, name="gate_t%d" % r) for r in range(2)]
+        wa_of = {e: wa_t[c][:, e - a, :] for c, (a, b) in enumerate(chunks) for e in range(a, b)}
+        ident1 = keep.tile([P, P], F32, name="ident1")
+        ident = keep.tile([P, P], F32, name="ident")
+
+        def load_scales(queue, plane, row0, scales):
+            for q in (0, 2, 1, 3):
+                queue.dma_start(
+                    out=plane[32 * q + row0 : 32 * q + row0 + 4, :, :].bitcast(I32),
+                    in_=scales[:, 0, 4 * q : 4 * q + 4, :].rearrange("e r n -> r e n").bitcast(I32),
+                )
+
+        def load_wa(c):
+            a, b = chunks[c]
+            nc.sync.dma_start(
+                out=wa_t[c][:], in_=wa_words[a:b, 0].rearrange("e p i d -> p e (i d)").bitcast(I32)
+            )
+
+        nc.vector.memset(wa_sc[:].rearrange("p e n -> p (e n)").bitcast(I32), 0)
+        make_identity(nc, ident1[:])
+        nc.vector.memset(wy_sc[:].rearrange("p e n -> p (e n)").bitcast(I32), 0)
+
+        nc.sync.dma_start(out=xw[:], in_=x_words[0].rearrange("p t d -> p (t d)").bitcast(I32))
+        nc.sync.dma_start(offs_t[:], offs)
+        for q in range(4):
+            nc.sync.dma_start(
+                out=xs[32 * q : 32 * q + 32, :].bitcast(I32),
+                in_=x_scales[0, 4 * q : 4 * q + 4, :].bitcast(I32).partition_broadcast(8),
+            )
+        load_wa(0)
+        load_scales(nc.sync, wa_sc, WA_ROW, wa_scales)
+        nc.scalar.activation(ident[:], ident1[:], ACT.Relu)
+        load_wa(1)
+        load_wa(2)
+        nc.sync.dma_start(pos_t[0][:], pos1)
+        load_scales(nc.sync, wy_sc, 0, w_scales)
+        load_wa(3)
+        load_wa(4)
+        load_scales(nc.sync, wy_sc, WB_ROW, wb_scales)
+
+        def load_tile(j):
+            nc.sync.dma_start(
+                out=wb_t[j][:],
+                in_=wb_words[:, 0, :, P * j : P * (j + 1), :].rearrange("e p n d -> p e (n d)").bitcast(I32),
+            )
+            nc.sync.dma_start(
+                out=w_t[j][:].bitcast(I32),
+                in_=w_words[:, 0, :, 2 * P * j : 2 * P * (j + 1)].rearrange("e p b -> p e b").bitcast(I32),
+            )
+
+        load_tile(0)
+        nc.sync.dma_start(pos_t[1][:], pos2)
+        for r in range(2):
+            nc.sync.dma_start(out=gate_t[r][:], in_=gate[r])
+        for j in range(1, NT):
+            load_tile(j)
+
+        gw = keep.tile([P, S], U32, name="gw", align_bytes=64)
+        gs = keep.tile([P, S], U8, name="gs", align_bytes=64)
+        hb = [keep.tile([P, H], BF16, name="hb%d" % e, align_bytes=64) for e in range(E)]
+        for q in range(PAIRS):
+            slots = slice(2 * C * q, 2 * C * (q + 1))
+            cols = offs_t[:, 16 * q : 16 * (q + 1)]
+            nc.vector.tensor_copy(gw[:, slots], xw[:].bitcast(U32).indirect(cols))
+            nc.vector.tensor_copy(gs[:, slots], xs[:].indirect(cols))
+            for e in (2 * q, 2 * q + 1):
+                mine = slice(C * e, C * (e + 1))
+                hp = psum.tile([P, H], F32, name="bank%d" % (e % 3))
+                nc.tensor.matmul_mx(
+                    out=hp[:],
+                    lhsT=gw[:, mine].bitcast(FP8X4),
+                    lhsT_scale=gs[:, mine],
+                    rhs=wa_of[e].bitcast(FP8X4),
+                    rhs_scale=wa_sc[WA_ROW:P, e, :],
+                    start=True,
+                    stop=True,
+                )
+                nc.scalar.activation(
+                    hb[e][:].rearrange("s (u p d) -> s u p d", u=2, d=2),
+                    hp[:].rearrange("s (p u d) -> s u p d", u=2, d=2),
+                    ACT.Relu,
+                )
+
+        hq = keep.tile([P, S], U32, name="hq", align_bytes=64)
+        hs = keep.tile([P, S], U8, name="hs", align_bytes=64)
+        hg = [keep.tile([P, 2 * C * 4], BF16, name="hg%d" % q, align_bytes=64) for q in range(PAIRS)]
+
+        def turn(q):
+            tp = psum.tile([P, 2, 2, C], F32, name="bank%d" % (3 + q % 5))
+            for a in range(2):
+                words = hb[2 * q + a][:].bitcast(F32)
+                for u in range(2):
+                    nc.tensor.transpose(tp[:, a, u, :], words[:, P * u : P * (u + 1)], ident[:])
+            dst = hg[q][:].bitcast(F32).rearrange("p (a s u) -> p a s u", a=2, u=2)
+            src = tp[:].rearrange("p a u s -> p a s u")
+            if q in SCALAR_PAIRS:
+                nc.scalar.copy(dst, src)
+            else:
+                nc.vector.tensor_copy(dst, src)
+
+        def quantise(q):
+            slots = slice(2 * C * q, 2 * C * (q + 1))
+            nc.vector.quantize_mx(out=hq[:, slots].bitcast(FP8X4), scales=hs[:, slots], in_=hg[q][:])
+
+        turn(0)
+        for q in range(1, PAIRS):
+            turn(q)
+            quantise(q - 1)
+        quantise(PAIRS - 1)
+
+        y = [keep.tile([P, S], F32, name="y%d" % j) for j in range(NT)]
+
+        def products(j):
+            cols = slice(P * j, P * (j + 1))
+            for b in range(E // 4):
+                yp = psum.tile([P, 4 * C], F32, name="bank%d" % (4 * (j % 2) + b))
+                for a in range(4):
+                    e = 4 * b + a
+                    mine = slice(C * e, C * (e + 1))
+                    nc.tensor.matmul_mx(
+                        out=yp[:, C * a : C * (a + 1)],
+                        lhsT=w_t[j][:, e, :].bitcast(FP4X4),
+                        lhsT_scale=wy_sc[:, e, cols],
+                        rhs=gw[:, mine].bitcast(FP8X4),
+                        rhs_scale=gs[:, mine],
+                        start=True,
+                        stop=False,
+                    )
+                    nc.tensor.matmul_mx(
+                        out=yp[:, C * a : C * (a + 1)],
+                        lhsT=wb_t[j][:, e, :].bitcast(FP8X4),
+                        lhsT_scale=wy_sc[WB_ROW:P, e, cols],
+                        rhs=hq[:, mine].bitcast(FP8X4),
+                        rhs_scale=hs[:, mine],
+                        start=False,
+                        stop=True,
+                    )
+                nc.scalar.copy(y[j][:, 4 * C * b : 4 * C * (b + 1)], yp[:])
+
+        pieces = [(j, 0, T) for j in range(NT - 1)]
+        pieces += [(NT - 1, a, b) for a, b in zip(LAST_CUTS[:-1], LAST_CUTS[1:])]
+
+        def fetch(r, j, t0, t1):
+            part = ring.tile([P, t1 - t0], F32, name="part%d" % r)
+            nc.vector.tensor_tensor(
+                part[:], y[j][:].indirect(pos_t[r][:, t0 // 16 : t1 // 16]), gate_t[r][:, t0:t1], MULT
+            )
+            return part
+
+        def finish(j, t0, t1, both):
+            res = ring.tile([P, t1 - t0], F32, name="res")
+            nc.vector.tensor_tensor(res[:], both[0][:], both[1][:], ADD)
+            nc.sync.dma_start(out=out[P * j : P * (j + 1), t0:t1], in_=res[:])
+
+        for j in range(NT):
+            products(j)
+        first = fetch(0, *pieces[0])
+        for i, piece in enumerate(pieces):
+            both = [first, fetch(1, *piece)]
+            if i + 1 < len(pieces):
+                first = fetch(0, *pieces[i + 1])
+            finish(*piece, both)

@@ -22,11 +22,12 @@ ADD = mybir.AluOpType.add
 
 NT = N // P
 PAIRS = E // 2
-WA_ROW = 4
 WB_ROW = 8
 SCALAR_PAIRS = (3, 4, 5)
 LAST_CUTS = (0, 512, 768)
-WA_CUTS = (0, 2, 5, 8, 10, 12)
+WA_CUTS = (0, 2, 4, 8, 12)
+TURN_BANK = (4, 5, 0, 1, 6, 7)
+Y_BANKS = ((2, 4, 3), (5, 0, 1), (6, 7, 2), (3, 4, 5))
 
 
 def tile_moe_elr_relu_kernel(
@@ -44,12 +45,12 @@ def tile_moe_elr_relu_kernel(
 
         xw = keep.tile([P, T], I32, name="xw", align_bytes=64)
         xs = keep.tile([P, T], U8, name="xs", align_bytes=64)
-        wa_sc = keep.tile([P, E, H], U8, name="wa_sc", align_bytes=64)
+        wa_sc = [keep.tile([P, H], U8, name="wa_sc%d" % g, align_bytes=64) for g in range(E // 4)]
         wy_sc = keep.tile([P, E, N], U8, name="wy_sc", align_bytes=64)
         chunks = list(zip(WA_CUTS[:-1], WA_CUTS[1:]))
         wa_t = [keep.tile([P, b - a, H], I32, name="wa_t%d" % a, align_bytes=64) for a, b in chunks]
         wb_t = [keep.tile([P, E, P], I32, name="wb_t%d" % j, align_bytes=64) for j in range(NT)]
-        w_t = [keep.tile([P, E, 2 * P], U8, name="w_t%d" % j, align_bytes=64) for j in range(NT)]
+        w_t = [keep.tile([P, E, 4 * P], U8, name="w_t%d" % j, align_bytes=64) for j in range(NT // 2)]
         gate_t = [keep.tile([P, T], F32, name="gate_t%d" % r) for r in range(2)]
         wa_of = {e: wa_t[c][:, e - a, :] for c, (a, b) in enumerate(chunks) for e in range(a, b)}
         ident1 = keep.tile([P, P], F32, name="ident1")
@@ -68,44 +69,58 @@ def tile_moe_elr_relu_kernel(
                 out=wa_t[c][:], in_=wa_words[a:b, 0].rearrange("e p i d -> p e (i d)").bitcast(I32)
             )
 
-        nc.vector.memset(wa_sc[:].rearrange("p e n -> p (e n)").bitcast(I32), 0)
+        def load_wa_scales(g):
+            for q in range(4):
+                nc.sync.dma_start(
+                    out=wa_sc[g][32 * q : 32 * q + 16, :].bitcast(I32),
+                    in_=wa_scales[4 * g : 4 * g + 4, 0, 4 * q : 4 * q + 4, :].bitcast(I32),
+                )
+
+        nc.vector.memset(xs[:].bitcast(I32), 0)
+        for g in range(E // 4):
+            nc.vector.memset(wa_sc[g][:].bitcast(I32), 0)
         make_identity(nc, ident1[:])
         nc.vector.memset(wy_sc[:].rearrange("p e n -> p (e n)").bitcast(I32), 0)
 
         nc.sync.dma_start(out=xw[:], in_=x_words[0].rearrange("p t d -> p (t d)").bitcast(I32))
-        nc.sync.dma_start(offs_t[:], offs)
-        for q in range(4):
+        for q in (0, 2, 1, 3):
             nc.sync.dma_start(
-                out=xs[32 * q : 32 * q + 32, :].bitcast(I32),
-                in_=x_scales[0, 4 * q : 4 * q + 4, :].bitcast(I32).partition_broadcast(8),
+                out=xs[32 * q : 32 * q + 4, :].bitcast(I32), in_=x_scales[0, 4 * q : 4 * q + 4, :].bitcast(I32)
             )
+        nc.sync.dma_start(offs_t[:], offs)
         load_wa(0)
-        load_scales(nc.sync, wa_sc, WA_ROW, wa_scales)
+        load_wa_scales(0)
         nc.scalar.activation(ident[:], ident1[:], ACT.Relu)
         load_wa(1)
         load_wa(2)
-        nc.sync.dma_start(pos_t[0][:], pos1)
-        load_scales(nc.sync, wy_sc, 0, w_scales)
+        load_wa_scales(1)
         load_wa(3)
-        load_wa(4)
-        load_scales(nc.sync, wy_sc, WB_ROW, wb_scales)
+        load_wa_scales(2)
+        load_scales(nc.gpsimd, wy_sc, WB_ROW, wb_scales)
+        load_scales(nc.gpsimd, wy_sc, 0, w_scales)
 
-        def load_tile(j):
+        def load_wb(j, a, b):
             nc.sync.dma_start(
-                out=wb_t[j][:],
-                in_=wb_words[:, 0, :, P * j : P * (j + 1), :].rearrange("e p n d -> p e (n d)").bitcast(I32),
-            )
-            nc.sync.dma_start(
-                out=w_t[j][:].bitcast(I32),
-                in_=w_words[:, 0, :, 2 * P * j : 2 * P * (j + 1)].rearrange("e p b -> p e b").bitcast(I32),
+                out=wb_t[j][:, a:b, :],
+                in_=wb_words[a:b, 0, :, P * j : P * (j + 1), :].rearrange("e p n d -> p e (n d)").bitcast(I32),
             )
 
-        load_tile(0)
-        nc.sync.dma_start(pos_t[1][:], pos2)
-        for r in range(2):
+        def load_w(jj, a, b):
+            nc.sync.dma_start(
+                out=w_t[jj][:, a:b, :].bitcast(I32),
+                in_=w_words[a:b, 0, :, 4 * P * jj : 4 * P * (jj + 1)].rearrange("e p b -> p e b").bitcast(I32),
+            )
+
+        for a, b in ((0, 8), (8, E)):
+            load_w(0, a, b)
+            load_wb(0, a, b)
+        for r, pos in enumerate((pos1, pos2)):
+            nc.sync.dma_start(pos_t[r][:], pos)
             nc.sync.dma_start(out=gate_t[r][:], in_=gate[r])
-        for j in range(1, NT):
-            load_tile(j)
+        load_wb(1, 0, E)
+        load_w(1, 0, E)
+        load_wb(2, 0, E)
+        load_wb(3, 0, E)
 
         gw = keep.tile([P, S], U32, name="gw", align_bytes=64)
         gs = keep.tile([P, S], U8, name="gs", align_bytes=64)
@@ -117,13 +132,13 @@ def tile_moe_elr_relu_kernel(
             nc.vector.tensor_copy(gs[:, slots], xs[:].indirect(cols))
             for e in (2 * q, 2 * q + 1):
                 mine = slice(C * e, C * (e + 1))
-                hp = psum.tile([P, H], F32, name="bank%d" % (e % 3))
+                hp = psum.tile([P, H], F32, name="bank%d" % (e % 8))
                 nc.tensor.matmul_mx(
                     out=hp[:],
                     lhsT=gw[:, mine].bitcast(FP8X4),
                     lhsT_scale=gs[:, mine],
                     rhs=wa_of[e].bitcast(FP8X4),
-                    rhs_scale=wa_sc[WA_ROW:P, e, :],
+                    rhs_scale=wa_sc[e // 4][4 * (e % 4) : P, :],
                     start=True,
                     stop=True,
                 )
@@ -138,7 +153,7 @@ def tile_moe_elr_relu_kernel(
         hg = [keep.tile([P, 2 * C * 4], BF16, name="hg%d" % q, align_bytes=64) for q in range(PAIRS)]
 
         def turn(q):
-            tp = psum.tile([P, 2, 2, C], F32, name="bank%d" % (3 + q % 5))
+            tp = psum.tile([P, 2, 2, C], F32, name="bank%d" % TURN_BANK[q])
             for a in range(2):
                 words = hb[2 * q + a][:].bitcast(F32)
                 for u in range(2):
@@ -165,13 +180,13 @@ def tile_moe_elr_relu_kernel(
         def products(j):
             cols = slice(P * j, P * (j + 1))
             for b in range(E // 4):
-                yp = psum.tile([P, 4 * C], F32, name="bank%d" % (4 * (j % 2) + b))
+                yp = psum.tile([P, 4 * C], F32, name="bank%d" % Y_BANKS[j][b])
                 for a in range(4):
                     e = 4 * b + a
                     mine = slice(C * e, C * (e + 1))
                     nc.tensor.matmul_mx(
                         out=yp[:, C * a : C * (a + 1)],
-                        lhsT=w_t[j][:, e, :].bitcast(FP4X4),
+                        lhsT=w_t[j // 2][:, e, 2 * P * (j % 2) : 2 * P * (j % 2 + 1)].bitcast(FP4X4),
                         lhsT_scale=wy_sc[:, e, cols],
                         rhs=gw[:, mine].bitcast(FP8X4),
                         rhs_scale=gs[:, mine],

@@ -23,11 +23,13 @@ ADD = mybir.AluOpType.add
 NT = N // P
 PAIRS = E // 2
 WB_ROW = 8
-SCALAR_PAIRS = (3, 4, 5)
+WA_ROW = 4
+SCALAR_PAIRS = (4, 5)
 LAST_CUTS = (0, 512, 768)
-WA_CUTS = (0, 2, 4, 8, 12)
+WA_CUTS = (0, 3, 6, 9, 12)
 TURN_BANK = (4, 5, 0, 1, 6, 7)
-Y_BANKS = ((2, 4, 3), (5, 0, 1), (6, 7, 2), (3, 4, 5))
+Y_BANKS = ((2, 4, 3, 5), (0, 1, 6), (7, 2, 4), (3, 5, 0))
+Y_CUTS = ((0, 4, 8, 10, 12), (0, 4, 8, 12), (0, 4, 8, 12), (0, 4, 8, 12))
 
 
 def tile_moe_elr_relu_kernel(
@@ -45,7 +47,7 @@ def tile_moe_elr_relu_kernel(
 
         xw = keep.tile([P, T], I32, name="xw", align_bytes=64)
         xs = keep.tile([P, T], U8, name="xs", align_bytes=64)
-        wa_sc = [keep.tile([P, H], U8, name="wa_sc%d" % g, align_bytes=64) for g in range(E // 4)]
+        wa_sc = keep.tile([P, E, H], U8, name="wa_sc", align_bytes=64)
         wy_sc = keep.tile([P, E, N], U8, name="wy_sc", align_bytes=64)
         chunks = list(zip(WA_CUTS[:-1], WA_CUTS[1:]))
         wa_t = [keep.tile([P, b - a, H], I32, name="wa_t%d" % a, align_bytes=64) for a, b in chunks]
@@ -57,11 +59,9 @@ def tile_moe_elr_relu_kernel(
         ident = keep.tile([P, P], F32, name="ident")
 
         def load_scales(queue, plane, row0, scales):
-            for q in (0, 2, 1, 3):
-                queue.dma_start(
-                    out=plane[32 * q + row0 : 32 * q + row0 + 4, :, :].bitcast(I32),
-                    in_=scales[:, 0, 4 * q : 4 * q + 4, :].rearrange("e r n -> r e n").bitcast(I32),
-                )
+            rows = scales[:, 0].rearrange("e (q r) n -> r q e n", r=4)
+            for r in range(4):
+                queue.dma_start(out=plane[row0 + r : P : 32, :, :].bitcast(I32), in_=rows[r].bitcast(I32))
 
         def load_wa(c):
             a, b = chunks[c]
@@ -69,35 +69,22 @@ def tile_moe_elr_relu_kernel(
                 out=wa_t[c][:], in_=wa_words[a:b, 0].rearrange("e p i d -> p e (i d)").bitcast(I32)
             )
 
-        def load_wa_scales(g):
-            for q in range(4):
-                nc.sync.dma_start(
-                    out=wa_sc[g][32 * q : 32 * q + 16, :].bitcast(I32),
-                    in_=wa_scales[4 * g : 4 * g + 4, 0, 4 * q : 4 * q + 4, :].bitcast(I32),
-                )
-
         nc.vector.memset(xs[:].bitcast(I32), 0)
-        for g in range(E // 4):
-            nc.vector.memset(wa_sc[g][:].bitcast(I32), 0)
+        nc.vector.memset(wa_sc[:].rearrange("p e n -> p (e n)").bitcast(I32), 0)
         make_identity(nc, ident1[:])
         nc.vector.memset(wy_sc[:].rearrange("p e n -> p (e n)").bitcast(I32), 0)
 
         nc.sync.dma_start(out=xw[:], in_=x_words[0].rearrange("p t d -> p (t d)").bitcast(I32))
-        for q in (0, 2, 1, 3):
-            nc.sync.dma_start(
-                out=xs[32 * q : 32 * q + 4, :].bitcast(I32), in_=x_scales[0, 4 * q : 4 * q + 4, :].bitcast(I32)
-            )
+        x_rows = x_scales[0].rearrange("(q r) t -> r q t", r=4)
+        for r in range(4):
+            nc.sync.dma_start(out=xs[r:P:32, :].bitcast(I32), in_=x_rows[r].bitcast(I32))
         nc.sync.dma_start(offs_t[:], offs)
-        load_wa(0)
-        load_wa_scales(0)
         nc.scalar.activation(ident[:], ident1[:], ACT.Relu)
-        load_wa(1)
-        load_wa(2)
-        load_wa_scales(1)
-        load_wa(3)
-        load_wa_scales(2)
-        load_scales(nc.gpsimd, wy_sc, WB_ROW, wb_scales)
+        for c in range(len(chunks)):
+            load_wa(c)
+        load_scales(nc.gpsimd, wa_sc, WA_ROW, wa_scales)
         load_scales(nc.gpsimd, wy_sc, 0, w_scales)
+        load_scales(nc.gpsimd, wy_sc, WB_ROW, wb_scales)
 
         def load_wb(j, a, b):
             nc.sync.dma_start(
@@ -111,16 +98,17 @@ def tile_moe_elr_relu_kernel(
                 in_=w_words[a:b, 0, :, 4 * P * jj : 4 * P * (jj + 1)].rearrange("e p b -> p e b").bitcast(I32),
             )
 
-        for a, b in ((0, 8), (8, E)):
-            load_w(0, a, b)
+        load_w(0, 0, E)
+        for a, b in ((0, 8), (8, 10), (10, E)):
             load_wb(0, a, b)
         for r, pos in enumerate((pos1, pos2)):
             nc.sync.dma_start(pos_t[r][:], pos)
             nc.sync.dma_start(out=gate_t[r][:], in_=gate[r])
-        load_wb(1, 0, E)
-        load_w(1, 0, E)
-        load_wb(2, 0, E)
-        load_wb(3, 0, E)
+        for j in range(1, NT):
+            if j % 2 == 0:
+                load_w(j // 2, 0, E)
+            for a, b in ((0, 8), (8, E)):
+                load_wb(j, a, b)
 
         gw = keep.tile([P, S], U32, name="gw", align_bytes=64)
         gs = keep.tile([P, S], U8, name="gs", align_bytes=64)
@@ -138,7 +126,7 @@ def tile_moe_elr_relu_kernel(
                     lhsT=gw[:, mine].bitcast(FP8X4),
                     lhsT_scale=gs[:, mine],
                     rhs=wa_of[e].bitcast(FP8X4),
-                    rhs_scale=wa_sc[e // 4][4 * (e % 4) : P, :],
+                    rhs_scale=wa_sc[WA_ROW:P, e, :],
                     start=True,
                     stop=True,
                 )
@@ -179,10 +167,10 @@ def tile_moe_elr_relu_kernel(
 
         def products(j):
             cols = slice(P * j, P * (j + 1))
-            for b in range(E // 4):
-                yp = psum.tile([P, 4 * C], F32, name="bank%d" % Y_BANKS[j][b])
-                for a in range(4):
-                    e = 4 * b + a
+            for b, (e0, e1) in enumerate(zip(Y_CUTS[j][:-1], Y_CUTS[j][1:])):
+                yp = psum.tile([P, (e1 - e0) * C], F32, name="bank%d" % Y_BANKS[j][b])
+                for e in range(e0, e1):
+                    a = e - e0
                     mine = slice(C * e, C * (e + 1))
                     nc.tensor.matmul_mx(
                         out=yp[:, C * a : C * (a + 1)],
@@ -202,7 +190,10 @@ def tile_moe_elr_relu_kernel(
                         start=False,
                         stop=True,
                     )
-                nc.scalar.copy(y[j][:, 4 * C * b : 4 * C * (b + 1)], yp[:])
+                if j == 0 and e1 == E:
+                    nc.vector.tensor_copy(y[j][:, C * e0 : C * e1], yp[:])
+                else:
+                    nc.scalar.copy(y[j][:, C * e0 : C * e1], yp[:])
 
         pieces = [(j, 0, T) for j in range(NT - 1)]
         pieces += [(NT - 1, a, b) for a, b in zip(LAST_CUTS[:-1], LAST_CUTS[1:])]

@@ -80,11 +80,11 @@ def tile_moe_elr_relu_kernel(
             nc.sync.dma_start(out=xs[r:P:32, :].bitcast(I32), in_=x_rows[r].bitcast(I32))
         nc.sync.dma_start(offs_t[:], offs)
         nc.scalar.activation(ident[:], ident1[:], ACT.Relu)
-        for c in range(len(chunks)):
+        load_wa(0)
+        load_scales(nc.sync, wa_sc, WA_ROW, wa_scales)
+        for c in range(1, len(chunks)):
             load_wa(c)
-        load_scales(nc.gpsimd, wa_sc, WA_ROW, wa_scales)
         load_scales(nc.gpsimd, wy_sc, 0, w_scales)
-        load_scales(nc.gpsimd, wy_sc, WB_ROW, wb_scales)
 
         def load_wb(j, a, b):
             nc.sync.dma_start(
@@ -99,6 +99,7 @@ def tile_moe_elr_relu_kernel(
             )
 
         load_w(0, 0, E)
+        load_scales(nc.sync, wy_sc, WB_ROW, wb_scales)
         for a, b in ((0, 8), (8, 10), (10, E)):
             load_wb(0, a, b)
         for r, pos in enumerate((pos1, pos2)):

@@ -22,14 +22,15 @@ ADD = mybir.AluOpType.add
 
 NT = N // P
 PAIRS = E // 2
+TB = T // P
+GATE_BANKS = (4, 5, 6, 7)
 WB_ROW = 8
-WA_ROW = 4
 SCALAR_PAIRS = (4, 5)
 LAST_CUTS = (0, 512, 768)
-WA_CUTS = (0, 3, 6, 9, 12)
+WA_CUTS = (0, 2, 4, 8, 12)
 TURN_BANK = (4, 5, 0, 1, 6, 7)
-Y_BANKS = ((2, 4, 3, 5), (0, 1, 6), (7, 2, 4), (3, 5, 0))
-Y_CUTS = ((0, 4, 8, 10, 12), (0, 4, 8, 12), (0, 4, 8, 12), (0, 4, 8, 12))
+Y_BANKS = ((2, 3, 4, 5), (0, 1, 6, 7))
+RUN = 4
 
 
 def tile_moe_elr_relu_kernel(
@@ -47,13 +48,15 @@ def tile_moe_elr_relu_kernel(
 
         xw = keep.tile([P, T], I32, name="xw", align_bytes=64)
         xs = keep.tile([P, T], U8, name="xs", align_bytes=64)
-        wa_sc = keep.tile([P, E, H], U8, name="wa_sc", align_bytes=64)
+        wa_sc = [keep.tile([P, H], U8, name="wa_sc%d" % g, align_bytes=64) for g in range(E // 4)]
         wy_sc = keep.tile([P, E, N], U8, name="wy_sc", align_bytes=64)
         chunks = list(zip(WA_CUTS[:-1], WA_CUTS[1:]))
         wa_t = [keep.tile([P, b - a, H], I32, name="wa_t%d" % a, align_bytes=64) for a, b in chunks]
         wb_t = [keep.tile([P, E, P], I32, name="wb_t%d" % j, align_bytes=64) for j in range(NT)]
         w_t = [keep.tile([P, E, 4 * P], U8, name="w_t%d" % j, align_bytes=64) for j in range(NT // 2)]
-        gate_t = [keep.tile([P, T], F32, name="gate_t%d" % r) for r in range(2)]
+        gate_rows = keep.tile([P, P], F32, name="gate_rows")
+        gate_cols = keep.tile([P, 2 * TB], F32, name="gate_cols")
+        gate_t = keep.tile([P, 2 * T], F32, name="gate_t")
         wa_of = {e: wa_t[c][:, e - a, :] for c, (a, b) in enumerate(chunks) for e in range(a, b)}
         ident1 = keep.tile([P, P], F32, name="ident1")
         ident = keep.tile([P, P], F32, name="ident")
@@ -69,8 +72,17 @@ def tile_moe_elr_relu_kernel(
                 out=wa_t[c][:], in_=wa_words[a:b, 0].rearrange("e p i d -> p e (i d)").bitcast(I32)
             )
 
+        def load_wa_scales(g):
+            for q in range(4):
+                nc.sync.dma_start(
+                    out=wa_sc[g][32 * q : 32 * q + 16, :].bitcast(I32),
+                    in_=wa_scales[4 * g : 4 * g + 4, 0, 4 * q : 4 * q + 4, :].bitcast(I32),
+                )
+
+        nc.vector.memset(gate_rows[:], 0.0)
         nc.vector.memset(xs[:].bitcast(I32), 0)
-        nc.vector.memset(wa_sc[:].rearrange("p e n -> p (e n)").bitcast(I32), 0)
+        for g in range(E // 4):
+            nc.vector.memset(wa_sc[g][:].bitcast(I32), 0)
         make_identity(nc, ident1[:])
         nc.vector.memset(wy_sc[:].rearrange("p e n -> p (e n)").bitcast(I32), 0)
 
@@ -79,12 +91,17 @@ def tile_moe_elr_relu_kernel(
         for r in range(4):
             nc.sync.dma_start(out=xs[r:P:32, :].bitcast(I32), in_=x_rows[r].bitcast(I32))
         nc.sync.dma_start(offs_t[:], offs)
+        nc.scalar.dma_start(out=gate_rows[: 2 * TB, :], in_=gate[:, 0, :].rearrange("r (m c) -> r m c", c=P))
         nc.scalar.activation(ident[:], ident1[:], ACT.Relu)
         load_wa(0)
-        load_scales(nc.sync, wa_sc, WA_ROW, wa_scales)
-        for c in range(1, len(chunks)):
-            load_wa(c)
+        load_wa_scales(0)
+        load_wa(1)
+        load_wa(2)
+        load_wa_scales(1)
+        load_wa(3)
+        load_wa_scales(2)
         load_scales(nc.gpsimd, wy_sc, 0, w_scales)
+        load_scales(nc.gpsimd, wy_sc, WB_ROW, wb_scales)
 
         def load_wb(j, a, b):
             nc.sync.dma_start(
@@ -99,17 +116,25 @@ def tile_moe_elr_relu_kernel(
             )
 
         load_w(0, 0, E)
-        load_scales(nc.sync, wy_sc, WB_ROW, wb_scales)
-        for a, b in ((0, 8), (8, 10), (10, E)):
+        for a, b in ((0, 8), (8, E)):
             load_wb(0, a, b)
         for r, pos in enumerate((pos1, pos2)):
             nc.sync.dma_start(pos_t[r][:], pos)
-            nc.sync.dma_start(out=gate_t[r][:], in_=gate[r])
         for j in range(1, NT):
             if j % 2 == 0:
                 load_w(j // 2, 0, E)
             for a, b in ((0, 8), (8, E)):
                 load_wb(j, a, b)
+
+        turned = psum.tile([P, P], F32, name="bank%d" % GATE_BANKS[0])
+        nc.tensor.transpose(turned[:], gate_rows[:], ident[:])
+        nc.scalar.copy(gate_cols[:], turned[:, : 2 * TB])
+        for b in range(2 * TB // 4):
+            spread = psum.tile([P, 4 * P], F32, name="bank%d" % GATE_BANKS[b + 1])
+            for a in range(4):
+                col = gate_cols[:, 4 * b + a : 4 * b + a + 1]
+                nc.tensor.transpose(spread[:, P * a : P * (a + 1)], col.to_broadcast([P, P]), ident[:])
+            nc.scalar.copy(gate_t[:, 4 * P * b : 4 * P * (b + 1)], spread[:])
 
         gw = keep.tile([P, S], U32, name="gw", align_bytes=64)
         gs = keep.tile([P, S], U8, name="gs", align_bytes=64)
@@ -127,7 +152,7 @@ def tile_moe_elr_relu_kernel(
                     lhsT=gw[:, mine].bitcast(FP8X4),
                     lhsT_scale=gs[:, mine],
                     rhs=wa_of[e].bitcast(FP8X4),
-                    rhs_scale=wa_sc[WA_ROW:P, e, :],
+                    rhs_scale=wa_sc[e // 4][4 * (e % 4) : P, :],
                     start=True,
                     stop=True,
                 )
@@ -168,13 +193,13 @@ def tile_moe_elr_relu_kernel(
 
         def products(j):
             cols = slice(P * j, P * (j + 1))
-            for b, (e0, e1) in enumerate(zip(Y_CUTS[j][:-1], Y_CUTS[j][1:])):
-                yp = psum.tile([P, (e1 - e0) * C], F32, name="bank%d" % Y_BANKS[j][b])
-                for e in range(e0, e1):
-                    a = e - e0
+            yp = [psum.tile([P, E // RUN, C], F32, name="bank%d" % bank) for bank in Y_BANKS[j % 2]]
+            for g in range(E // RUN):
+                for b in range(RUN):
+                    e = RUN * g + b
                     mine = slice(C * e, C * (e + 1))
                     nc.tensor.matmul_mx(
-                        out=yp[:, C * a : C * (a + 1)],
+                        out=yp[b][:, g, :],
                         lhsT=w_t[j // 2][:, e, 2 * P * (j % 2) : 2 * P * (j % 2 + 1)].bitcast(FP4X4),
                         lhsT_scale=wy_sc[:, e, cols],
                         rhs=gw[:, mine].bitcast(FP8X4),
@@ -182,8 +207,11 @@ def tile_moe_elr_relu_kernel(
                         start=True,
                         stop=False,
                     )
+                for b in range(RUN):
+                    e = RUN * g + b
+                    mine = slice(C * e, C * (e + 1))
                     nc.tensor.matmul_mx(
-                        out=yp[:, C * a : C * (a + 1)],
+                        out=yp[b][:, g, :],
                         lhsT=wb_t[j][:, e, :].bitcast(FP8X4),
                         lhsT_scale=wy_sc[WB_ROW:P, e, cols],
                         rhs=hq[:, mine].bitcast(FP8X4),
@@ -191,10 +219,12 @@ def tile_moe_elr_relu_kernel(
                         start=False,
                         stop=True,
                     )
-                if j == 0 and e1 == E:
-                    nc.vector.tensor_copy(y[j][:, C * e0 : C * e1], yp[:])
+            by_bank = y[j][:].rearrange("p (g b c) -> p b g c", b=RUN, c=C)
+            for b in range(RUN):
+                if j == 0 and b % 2 == 1:
+                    nc.vector.tensor_copy(by_bank[:, b], yp[b][:])
                 else:
-                    nc.scalar.copy(y[j][:, C * e0 : C * e1], yp[:])
+                    nc.scalar.copy(by_bank[:, b], yp[b][:])
 
         pieces = [(j, 0, T) for j in range(NT - 1)]
         pieces += [(NT - 1, a, b) for a, b in zip(LAST_CUTS[:-1], LAST_CUTS[1:])]
@@ -202,7 +232,7 @@ def tile_moe_elr_relu_kernel(
         def fetch(r, j, t0, t1):
             part = ring.tile([P, t1 - t0], F32, name="part%d" % r)
             nc.vector.tensor_tensor(
-                part[:], y[j][:].indirect(pos_t[r][:, t0 // 16 : t1 // 16]), gate_t[r][:, t0:t1], MULT
+                part[:], y[j][:].indirect(pos_t[r][:, t0 // 16 : t1 // 16]), gate_t[:, T * r + t0 : T * r + t1], MULT
             )
             return part
 

@@ -25,12 +25,12 @@ PAIRS = E // 2
 TB = T // P
 GATE_BANKS = (4, 5, 6, 7)
 WB_ROW = 8
-SCALAR_PAIRS = (4, 5)
+SCALAR_PAIRS = (3, 4, 5)
 LAST_CUTS = (0, 512, 768)
-WA_CUTS = (0, 2, 4, 8, 12)
+WA_CUTS = (0, 2, 4, 8, 10, 12)
 TURN_BANK = (4, 5, 0, 1, 6, 7)
-Y_BANKS = ((2, 3, 4, 5), (0, 1, 6, 7))
-RUN = 4
+Y_BANKS = ((2, 4, 3, 5), (0, 1, 6), (7, 2, 4), (3, 5, 0))
+Y_CUTS = ((0, 4, 8, 10, 12), (0, 4, 8, 12), (0, 4, 8, 12), (0, 4, 8, 12))
 
 
 def tile_moe_elr_relu_kernel(
@@ -83,23 +83,23 @@ def tile_moe_elr_relu_kernel(
         nc.vector.memset(xs[:].bitcast(I32), 0)
         for g in range(E // 4):
             nc.vector.memset(wa_sc[g][:].bitcast(I32), 0)
-        make_identity(nc, ident1[:])
         nc.vector.memset(wy_sc[:].rearrange("p e n -> p (e n)").bitcast(I32), 0)
+        make_identity(nc, ident1[:])
 
         nc.sync.dma_start(out=xw[:], in_=x_words[0].rearrange("p t d -> p (t d)").bitcast(I32))
-        x_rows = x_scales[0].rearrange("(q r) t -> r q t", r=4)
-        for r in range(4):
-            nc.sync.dma_start(out=xs[r:P:32, :].bitcast(I32), in_=x_rows[r].bitcast(I32))
-        nc.sync.dma_start(offs_t[:], offs)
         nc.scalar.dma_start(out=gate_rows[: 2 * TB, :], in_=gate[:, 0, :].rearrange("r (m c) -> r m c", c=P))
         nc.scalar.activation(ident[:], ident1[:], ACT.Relu)
         load_wa(0)
-        load_wa_scales(0)
         load_wa(1)
+        x_rows = x_scales[0].rearrange("(q r) t -> r q t", r=4)
+        for r in range(4):
+            nc.sync.dma_start(out=xs[r:P:32, :].bitcast(I32), in_=x_rows[r].bitcast(I32))
         load_wa(2)
-        load_wa_scales(1)
-        load_wa(3)
-        load_wa_scales(2)
+        nc.sync.dma_start(offs_t[:], offs)
+        load_wa_scales(0)
+        for g in range(1, E // 4):
+            load_wa(2 + g)
+            load_wa_scales(g)
         load_scales(nc.gpsimd, wy_sc, 0, w_scales)
         load_scales(nc.gpsimd, wy_sc, WB_ROW, wb_scales)
 
@@ -116,7 +116,7 @@ def tile_moe_elr_relu_kernel(
             )
 
         load_w(0, 0, E)
-        for a, b in ((0, 8), (8, E)):
+        for a, b in ((0, 8), (8, 10), (10, E)):
             load_wb(0, a, b)
         for r, pos in enumerate((pos1, pos2)):
             nc.sync.dma_start(pos_t[r][:], pos)
@@ -193,13 +193,13 @@ def tile_moe_elr_relu_kernel(
 
         def products(j):
             cols = slice(P * j, P * (j + 1))
-            yp = [psum.tile([P, E // RUN, C], F32, name="bank%d" % bank) for bank in Y_BANKS[j % 2]]
-            for g in range(E // RUN):
-                for b in range(RUN):
-                    e = RUN * g + b
+            for b, (e0, e1) in enumerate(zip(Y_CUTS[j][:-1], Y_CUTS[j][1:])):
+                yp = psum.tile([P, (e1 - e0) * C], F32, name="bank%d" % Y_BANKS[j][b])
+                for e in range(e0, e1):
+                    a = e - e0
                     mine = slice(C * e, C * (e + 1))
                     nc.tensor.matmul_mx(
-                        out=yp[b][:, g, :],
+                        out=yp[:, C * a : C * (a + 1)],
                         lhsT=w_t[j // 2][:, e, 2 * P * (j % 2) : 2 * P * (j % 2 + 1)].bitcast(FP4X4),
                         lhsT_scale=wy_sc[:, e, cols],
                         rhs=gw[:, mine].bitcast(FP8X4),
@@ -207,11 +207,8 @@ def tile_moe_elr_relu_kernel(
                         start=True,
                         stop=False,
                     )
-                for b in range(RUN):
-                    e = RUN * g + b
-                    mine = slice(C * e, C * (e + 1))
                     nc.tensor.matmul_mx(
-                        out=yp[b][:, g, :],
+                        out=yp[:, C * a : C * (a + 1)],
                         lhsT=wb_t[j][:, e, :].bitcast(FP8X4),
                         lhsT_scale=wy_sc[WB_ROW:P, e, cols],
                         rhs=hq[:, mine].bitcast(FP8X4),
@@ -219,12 +216,10 @@ def tile_moe_elr_relu_kernel(
                         start=False,
                         stop=True,
                     )
-            by_bank = y[j][:].rearrange("p (g b c) -> p b g c", b=RUN, c=C)
-            for b in range(RUN):
-                if j == 0 and b % 2 == 1:
-                    nc.vector.tensor_copy(by_bank[:, b], yp[b][:])
+                if j == 0 and e1 == E:
+                    nc.vector.tensor_copy(y[j][:, C * e0 : C * e1], yp[:])
                 else:
-                    nc.scalar.copy(by_bank[:, b], yp[b][:])
+                    nc.scalar.copy(y[j][:, C * e0 : C * e1], yp[:])
 
         pieces = [(j, 0, T) for j in range(NT - 1)]
         pieces += [(NT - 1, a, b) for a, b in zip(LAST_CUTS[:-1], LAST_CUTS[1:])]

@@ -27,7 +27,8 @@ GATE_BANKS = (4, 5, 6, 7)
 WB_ROW = 8
 SCALAR_PAIRS = (3, 4, 5)
 LAST_CUTS = (0, 512, 768)
-WA_CUTS = (0, 2, 4, 8, 10, 12)
+WA_CUTS = (0, 3, 6, 9, 12)
+WA_ROW = 4
 TURN_BANK = (4, 5, 0, 1, 6, 7)
 Y_BANKS = ((2, 4, 3, 5), (0, 1, 6), (7, 2, 4), (3, 5, 0))
 Y_CUTS = ((0, 4, 8, 10, 12), (0, 4, 8, 12), (0, 4, 8, 12), (0, 4, 8, 12))
@@ -48,7 +49,7 @@ def tile_moe_elr_relu_kernel(
 
         xw = keep.tile([P, T], I32, name="xw", align_bytes=64)
         xs = keep.tile([P, T], U8, name="xs", align_bytes=64)
-        wa_sc = [keep.tile([P, H], U8, name="wa_sc%d" % g, align_bytes=64) for g in range(E // 4)]
+        wa_sc = keep.tile([P, E, H], U8, name="wa_sc", align_bytes=64)
         wy_sc = keep.tile([P, E, N], U8, name="wy_sc", align_bytes=64)
         chunks = list(zip(WA_CUTS[:-1], WA_CUTS[1:]))
         wa_t = [keep.tile([P, b - a, H], I32, name="wa_t%d" % a, align_bytes=64) for a, b in chunks]
@@ -72,34 +73,26 @@ def tile_moe_elr_relu_kernel(
                 out=wa_t[c][:], in_=wa_words[a:b, 0].rearrange("e p i d -> p e (i d)").bitcast(I32)
             )
 
-        def load_wa_scales(g):
-            for q in range(4):
-                nc.sync.dma_start(
-                    out=wa_sc[g][32 * q : 32 * q + 16, :].bitcast(I32),
-                    in_=wa_scales[4 * g : 4 * g + 4, 0, 4 * q : 4 * q + 4, :].bitcast(I32),
-                )
-
         nc.vector.memset(gate_rows[:], 0.0)
+        nc.vector.memset(wa_sc[:].rearrange("p e n -> p (e n)").bitcast(I32), 0)
         nc.vector.memset(xs[:].bitcast(I32), 0)
-        for g in range(E // 4):
-            nc.vector.memset(wa_sc[g][:].bitcast(I32), 0)
         nc.vector.memset(wy_sc[:].rearrange("p e n -> p (e n)").bitcast(I32), 0)
         make_identity(nc, ident1[:])
-
-        nc.sync.dma_start(out=xw[:], in_=x_words[0].rearrange("p t d -> p (t d)").bitcast(I32))
-        nc.scalar.dma_start(out=gate_rows[: 2 * TB, :], in_=gate[:, 0, :].rearrange("r (m c) -> r m c", c=P))
         nc.scalar.activation(ident[:], ident1[:], ACT.Relu)
-        load_wa(0)
-        load_wa(1)
+
+        x_cols = x_words[0].rearrange("p t d -> p (t d)").bitcast(I32)
+        for half in (slice(0, T // 2), slice(T // 2, T)):
+            nc.sync.dma_start(out=xw[:, half], in_=x_cols[:, half])
+        for r, pos in enumerate((pos1, pos2)):
+            nc.sync.dma_start(pos_t[r][:], pos)
+        nc.sync.dma_start(offs_t[:], offs)
+        load_scales(nc.sync, wa_sc, WA_ROW, wa_scales)
         x_rows = x_scales[0].rearrange("(q r) t -> r q t", r=4)
         for r in range(4):
             nc.sync.dma_start(out=xs[r:P:32, :].bitcast(I32), in_=x_rows[r].bitcast(I32))
-        load_wa(2)
-        nc.sync.dma_start(offs_t[:], offs)
-        load_wa_scales(0)
-        for g in range(1, E // 4):
-            load_wa(2 + g)
-            load_wa_scales(g)
+        for c in range(len(chunks)):
+            load_wa(c)
+        nc.gpsimd.dma_start(out=gate_rows[: 2 * TB, :], in_=gate[:, 0, :].rearrange("r (m c) -> r m c", c=P))
         load_scales(nc.gpsimd, wy_sc, 0, w_scales)
         load_scales(nc.gpsimd, wy_sc, WB_ROW, wb_scales)
 
@@ -118,8 +111,6 @@ def tile_moe_elr_relu_kernel(
         load_w(0, 0, E)
         for a, b in ((0, 8), (8, 10), (10, E)):
             load_wb(0, a, b)
-        for r, pos in enumerate((pos1, pos2)):
-            nc.sync.dma_start(pos_t[r][:], pos)
         for j in range(1, NT):
             if j % 2 == 0:
                 load_w(j // 2, 0, E)
@@ -152,7 +143,7 @@ def tile_moe_elr_relu_kernel(
                     lhsT=gw[:, mine].bitcast(FP8X4),
                     lhsT_scale=gs[:, mine],
                     rhs=wa_of[e].bitcast(FP8X4),
-                    rhs_scale=wa_sc[e // 4][4 * (e % 4) : P, :],
+                    rhs_scale=wa_sc[WA_ROW:P, e, :],
                     start=True,
                     stop=True,
                 )

@@ -23,15 +23,21 @@ ADD = mybir.AluOpType.add
 NT = N // P
 PAIRS = E // 2
 TB = T // P
-GATE_BANKS = (4, 5, 6, 7)
-WB_ROW = 8
-SCALAR_PAIRS = (3, 4, 5)
+PACK = 4
+GROUPS = E // PACK
+SCALAR_PAIRS = (0, 5)
 LAST_CUTS = (0, 512, 768)
-WA_CUTS = (0, 3, 6, 9, 12)
-WA_ROW = 4
-TURN_BANK = (4, 5, 0, 1, 6, 7)
-Y_BANKS = ((2, 4, 3, 5), (0, 1, 6), (7, 2, 4), (3, 5, 0))
+WA_CUTS = (0, 4, 8, 12)
+H_BANKS = 8
+WB_ROW = 8
+TURN_BANK = (2, 4, 5, 0, 1, 6)
+GATE_BANKS = ((1, 2), (7, 4))
+Y_BANKS = ((7, 4, 5, 2), (3, 0, 1), (6, 5, 2), (7, 4, 3))
 Y_CUTS = ((0, 4, 8, 10, 12), (0, 4, 8, 12), (0, 4, 8, 12), (0, 4, 8, 12))
+
+
+def spans(cuts):
+    return list(zip(cuts[:-1], cuts[1:]))
 
 
 def tile_moe_elr_relu_kernel(
@@ -49,101 +55,123 @@ def tile_moe_elr_relu_kernel(
 
         xw = keep.tile([P, T], I32, name="xw", align_bytes=64)
         xs = keep.tile([P, T], U8, name="xs", align_bytes=64)
-        wa_sc = keep.tile([P, E, H], U8, name="wa_sc", align_bytes=64)
-        wy_sc = keep.tile([P, E, N], U8, name="wy_sc", align_bytes=64)
-        chunks = list(zip(WA_CUTS[:-1], WA_CUTS[1:]))
-        wa_t = [keep.tile([P, b - a, H], I32, name="wa_t%d" % a, align_bytes=64) for a, b in chunks]
-        wb_t = [keep.tile([P, E, P], I32, name="wb_t%d" % j, align_bytes=64) for j in range(NT)]
-        w_t = [keep.tile([P, E, 4 * P], U8, name="w_t%d" % j, align_bytes=64) for j in range(NT // 2)]
-        gate_rows = keep.tile([P, P], F32, name="gate_rows")
-        gate_cols = keep.tile([P, 2 * TB], F32, name="gate_cols")
-        gate_t = keep.tile([P, 2 * T], F32, name="gate_t")
-        wa_of = {e: wa_t[c][:, e - a, :] for c, (a, b) in enumerate(chunks) for e in range(a, b)}
+        wa_sc = [keep.tile([P, H], U8, name="wa_sc%d" % g, align_bytes=64) for g in range(GROUPS)]
+        wy_sc = [keep.tile([P, E, N // 2], U8, name="wy_sc%d" % h, align_bytes=64) for h in range(2)]
+        gate_rows = keep.tile([P, T // 2], F32, name="gate_rows")
+        gate_cols = keep.tile([P, TB // 2, 4], F32, name="gate_cols")
+        gate_t = [keep.tile([P, T], F32, name="gate_t%d" % r) for r in range(2)]
         ident1 = keep.tile([P, P], F32, name="ident1")
         ident = keep.tile([P, P], F32, name="ident")
+        wa_of, w_of, wb_of = {}, {}, {}
 
-        def load_scales(queue, plane, row0, scales):
-            rows = scales[:, 0].rearrange("e (q r) n -> r q e n", r=4)
+        def load_packed(g):
+            for quad in (0, 2, 1, 3):
+                nc.sync.dma_start(
+                    out=wa_sc[g][32 * quad : 32 * quad + 4 * PACK, :].bitcast(I32),
+                    in_=wa_scales[PACK * g : PACK * (g + 1), 0, 4 * quad : 4 * quad + 4, :].bitcast(I32),
+                )
+
+        def load_stepped(row0, scales, half):
+            cols = slice(N // 2 * half, N // 2 * (half + 1))
+            rows = scales[:, 0, :, cols].rearrange("e (q r) n -> r q e n", r=4)
             for r in range(4):
-                queue.dma_start(out=plane[row0 + r : P : 32, :, :].bitcast(I32), in_=rows[r].bitcast(I32))
+                nc.sync.dma_start(out=wy_sc[half][row0 + r : P : 32, :, :].bitcast(I32), in_=rows[r].bitcast(I32))
 
-        def load_wa(c):
-            a, b = chunks[c]
+        def load_wa(a, b):
+            words = keep.tile([P, b - a, H], I32, name="wa_t%d" % a, align_bytes=64)
+            nc.sync.dma_start(out=words[:], in_=wa_words[a:b, 0].rearrange("e p i d -> p e (i d)").bitcast(I32))
+            wa_of.update({e: words[:, e - a, :] for e in range(a, b)})
+
+        def load_wb(j, a, b):
+            words = keep.tile([P, b - a, P], I32, name="wb_t%d_%d" % (j, a), align_bytes=64)
             nc.sync.dma_start(
-                out=wa_t[c][:], in_=wa_words[a:b, 0].rearrange("e p i d -> p e (i d)").bitcast(I32)
+                out=words[:],
+                in_=wb_words[a:b, 0, :, P * j : P * (j + 1), :].rearrange("e p n d -> p e (n d)").bitcast(I32),
             )
+            wb_of.update({(j, e): words[:, e - a, :] for e in range(a, b)})
 
-        nc.vector.memset(gate_rows[:], 0.0)
-        nc.vector.memset(wa_sc[:].rearrange("p e n -> p (e n)").bitcast(I32), 0)
-        nc.vector.memset(xs[:].bitcast(I32), 0)
-        nc.vector.memset(wy_sc[:].rearrange("p e n -> p (e n)").bitcast(I32), 0)
+        def load_w(j0, j1, a, b):
+            words = keep.tile([P, b - a, 2 * P * (j1 - j0)], U8, name="w_t%d_%d" % (j0, a), align_bytes=64)
+            nc.sync.dma_start(
+                out=words[:].bitcast(I32),
+                in_=w_words[a:b, 0, :, 2 * P * j0 : 2 * P * j1].rearrange("e p b -> p e b").bitcast(I32),
+            )
+            for j in range(j0, j1):
+                w_of.update({(j, e): words[:, e - a, 2 * P * (j - j0) : 2 * P * (j - j0 + 1)] for e in range(a, b)})
+
+        nc.gpsimd.memset(xs[:].bitcast(I32), 0)
+        for plane in wa_sc:
+            nc.vector.memset(plane[:].bitcast(I32), 0)
+        for plane in wy_sc:
+            nc.vector.memset(plane[:].rearrange("p e n -> p (e n)").bitcast(I32), 0)
+        nc.gpsimd.memset(gate_rows[:], 0.0)
         make_identity(nc, ident1[:])
         nc.scalar.activation(ident[:], ident1[:], ACT.Relu)
 
-        x_cols = x_words[0].rearrange("p t d -> p (t d)").bitcast(I32)
-        for half in (slice(0, T // 2), slice(T // 2, T)):
-            nc.sync.dma_start(out=xw[:, half], in_=x_cols[:, half])
-        for r, pos in enumerate((pos1, pos2)):
-            nc.sync.dma_start(pos_t[r][:], pos)
-        nc.sync.dma_start(offs_t[:], offs)
-        load_scales(nc.sync, wa_sc, WA_ROW, wa_scales)
+        nc.sync.dma_start(out=xw[:], in_=x_words[0].rearrange("p t d -> p (t d)").bitcast(I32))
         x_rows = x_scales[0].rearrange("(q r) t -> r q t", r=4)
         for r in range(4):
             nc.sync.dma_start(out=xs[r:P:32, :].bitcast(I32), in_=x_rows[r].bitcast(I32))
-        for c in range(len(chunks)):
-            load_wa(c)
-        nc.gpsimd.dma_start(out=gate_rows[: 2 * TB, :], in_=gate[:, 0, :].rearrange("r (m c) -> r m c", c=P))
-        load_scales(nc.gpsimd, wy_sc, 0, w_scales)
-        load_scales(nc.gpsimd, wy_sc, WB_ROW, wb_scales)
-
-        def load_wb(j, a, b):
-            nc.sync.dma_start(
-                out=wb_t[j][:, a:b, :],
-                in_=wb_words[a:b, 0, :, P * j : P * (j + 1), :].rearrange("e p n d -> p e (n d)").bitcast(I32),
-            )
-
-        def load_w(jj, a, b):
-            nc.sync.dma_start(
-                out=w_t[jj][:, a:b, :].bitcast(I32),
-                in_=w_words[a:b, 0, :, 4 * P * jj : 4 * P * (jj + 1)].rearrange("e p b -> p e b").bitcast(I32),
-            )
-
-        load_w(0, 0, E)
-        for a, b in ((0, 8), (8, 10), (10, E)):
-            load_wb(0, a, b)
-        for j in range(1, NT):
-            if j % 2 == 0:
-                load_w(j // 2, 0, E)
+        nc.sync.dma_start(offs_t[:], offs)
+        nc.sync.dma_start(out=gate_rows[:4, :], in_=gate[:, 0, :].rearrange("r (h c) -> r h c", h=2))
+        for a, b in spans(WA_CUTS):
+            load_wa(a, b)
+            if a % PACK == 0:
+                load_packed(a // PACK)
+        load_w(0, 2, 0, E)
+        load_stepped(0, w_scales, 0)
+        load_wb(0, 0, 4)
+        load_stepped(WB_ROW, wb_scales, 0)
+        load_wb(0, 4, 8)
+        load_wb(0, 8, E)
+        for r, pos in enumerate((pos1, pos2)):
+            nc.sync.dma_start(pos_t[r][:], pos)
+        load_wb(1, 0, 8)
+        load_wb(1, 8, E)
+        load_stepped(0, w_scales, 1)
+        load_w(2, NT, 0, E)
+        load_stepped(WB_ROW, wb_scales, 1)
+        for j in range(2, NT):
             for a, b in ((0, 8), (8, E)):
                 load_wb(j, a, b)
 
-        turned = psum.tile([P, P], F32, name="bank%d" % GATE_BANKS[0])
-        nc.tensor.transpose(turned[:], gate_rows[:], ident[:])
-        nc.scalar.copy(gate_cols[:], turned[:, : 2 * TB])
-        for b in range(2 * TB // 4):
-            spread = psum.tile([P, 4 * P], F32, name="bank%d" % GATE_BANKS[b + 1])
-            for a in range(4):
-                col = gate_cols[:, 4 * b + a : 4 * b + a + 1]
-                nc.tensor.transpose(spread[:, P * a : P * (a + 1)], col.to_broadcast([P, P]), ident[:])
-            nc.scalar.copy(gate_t[:, 4 * P * b : 4 * P * (b + 1)], spread[:])
+        turned = psum.tile([P, TB // 2, P], F32, name="bank0")
+        for w in range(TB // 2):
+            nc.tensor.transpose(turned[:, w, :], gate_rows[:, P * w : P * (w + 1)], ident[:])
+        nc.scalar.copy(gate_cols[:], turned[:, :, :4])
+
+        def spread_gate(r):
+            for bank, (m0, m1) in zip(GATE_BANKS[r], ((0, 4), (4, TB))):
+                spread = psum.tile([P, (m1 - m0) * P], F32, name="bank%d" % bank)
+                for m in range(m0, m1):
+                    row = 2 * r + m // 3
+                    col = gate_cols[:, m % 3, row : row + 1]
+                    nc.tensor.transpose(spread[:, P * (m - m0) : P * (m - m0 + 1)], col.to_broadcast([P, P]), ident[:])
+                nc.scalar.copy(gate_t[r][:, P * m0 : P * m1], spread[:])
+
+        spread_gate(0)
 
         gw = keep.tile([P, S], U32, name="gw", align_bytes=64)
         gs = keep.tile([P, S], U8, name="gs", align_bytes=64)
         hb = [keep.tile([P, H], BF16, name="hb%d" % e, align_bytes=64) for e in range(E)]
-        for q in range(PAIRS):
+        hq = keep.tile([P, S], U32, name="hq", align_bytes=64)
+        hs = keep.tile([P, S], U8, name="hs", align_bytes=64)
+        hg = [keep.tile([P, 2 * C * 4], BF16, name="hg%d" % q, align_bytes=64) for q in range(PAIRS)]
+
+        def hidden(q):
             slots = slice(2 * C * q, 2 * C * (q + 1))
             cols = offs_t[:, 16 * q : 16 * (q + 1)]
             nc.vector.tensor_copy(gw[:, slots], xw[:].bitcast(U32).indirect(cols))
             nc.vector.tensor_copy(gs[:, slots], xs[:].indirect(cols))
             for e in (2 * q, 2 * q + 1):
                 mine = slice(C * e, C * (e + 1))
-                hp = psum.tile([P, H], F32, name="bank%d" % (e % 8))
+                hp = psum.tile([P, H], F32, name="bank%d" % (e % H_BANKS))
                 nc.tensor.matmul_mx(
                     out=hp[:],
                     lhsT=gw[:, mine].bitcast(FP8X4),
                     lhsT_scale=gs[:, mine],
                     rhs=wa_of[e].bitcast(FP8X4),
-                    rhs_scale=wa_sc[WA_ROW:P, e, :],
+                    rhs_scale=wa_sc[e // PACK][4 * (e % PACK) : P, :],
                     start=True,
                     stop=True,
                 )
@@ -152,10 +180,6 @@ def tile_moe_elr_relu_kernel(
                     hp[:].rearrange("s (p u d) -> s u p d", u=2, d=2),
                     ACT.Relu,
                 )
-
-        hq = keep.tile([P, S], U32, name="hq", align_bytes=64)
-        hs = keep.tile([P, S], U8, name="hs", align_bytes=64)
-        hg = [keep.tile([P, 2 * C * 4], BF16, name="hg%d" % q, align_bytes=64) for q in range(PAIRS)]
 
         def turn(q):
             tp = psum.tile([P, 2, 2, C], F32, name="bank%d" % TURN_BANK[q])
@@ -174,6 +198,8 @@ def tile_moe_elr_relu_kernel(
             slots = slice(2 * C * q, 2 * C * (q + 1))
             nc.vector.quantize_mx(out=hq[:, slots].bitcast(FP8X4), scales=hs[:, slots], in_=hg[q][:])
 
+        for q in range(PAIRS):
+            hidden(q)
         turn(0)
         for q in range(1, PAIRS):
             turn(q)
@@ -183,16 +209,16 @@ def tile_moe_elr_relu_kernel(
         y = [keep.tile([P, S], F32, name="y%d" % j) for j in range(NT)]
 
         def products(j):
-            cols = slice(P * j, P * (j + 1))
-            for b, (e0, e1) in enumerate(zip(Y_CUTS[j][:-1], Y_CUTS[j][1:])):
+            cols = slice(P * (j % 2), P * (j % 2 + 1))
+            for b, (e0, e1) in enumerate(spans(Y_CUTS[j])):
                 yp = psum.tile([P, (e1 - e0) * C], F32, name="bank%d" % Y_BANKS[j][b])
                 for e in range(e0, e1):
                     a = e - e0
                     mine = slice(C * e, C * (e + 1))
                     nc.tensor.matmul_mx(
                         out=yp[:, C * a : C * (a + 1)],
-                        lhsT=w_t[j // 2][:, e, 2 * P * (j % 2) : 2 * P * (j % 2 + 1)].bitcast(FP4X4),
-                        lhsT_scale=wy_sc[:, e, cols],
+                        lhsT=w_of[j, e].bitcast(FP4X4),
+                        lhsT_scale=wy_sc[j // 2][:, e, cols],
                         rhs=gw[:, mine].bitcast(FP8X4),
                         rhs_scale=gs[:, mine],
                         start=True,
@@ -200,8 +226,8 @@ def tile_moe_elr_relu_kernel(
                     )
                     nc.tensor.matmul_mx(
                         out=yp[:, C * a : C * (a + 1)],
-                        lhsT=wb_t[j][:, e, :].bitcast(FP8X4),
-                        lhsT_scale=wy_sc[WB_ROW:P, e, cols],
+                        lhsT=wb_of[j, e].bitcast(FP8X4),
+                        lhsT_scale=wy_sc[j // 2][WB_ROW:P, e, cols],
                         rhs=hq[:, mine].bitcast(FP8X4),
                         rhs_scale=hs[:, mine],
                         start=False,
@@ -213,12 +239,12 @@ def tile_moe_elr_relu_kernel(
                     nc.scalar.copy(y[j][:, C * e0 : C * e1], yp[:])
 
         pieces = [(j, 0, T) for j in range(NT - 1)]
-        pieces += [(NT - 1, a, b) for a, b in zip(LAST_CUTS[:-1], LAST_CUTS[1:])]
+        pieces += [(NT - 1, a, b) for a, b in spans(LAST_CUTS)]
 
         def fetch(r, j, t0, t1):
             part = ring.tile([P, t1 - t0], F32, name="part%d" % r)
             nc.vector.tensor_tensor(
-                part[:], y[j][:].indirect(pos_t[r][:, t0 // 16 : t1 // 16]), gate_t[:, T * r + t0 : T * r + t1], MULT
+                part[:], y[j][:].indirect(pos_t[r][:, t0 // 16 : t1 // 16]), gate_t[r][:, t0:t1], MULT
             )
             return part
 
@@ -227,7 +253,9 @@ def tile_moe_elr_relu_kernel(
             nc.vector.tensor_tensor(res[:], both[0][:], both[1][:], ADD)
             nc.sync.dma_start(out=out[P * j : P * (j + 1), t0:t1], in_=res[:])
 
-        for j in range(NT):
+        products(0)
+        spread_gate(1)
+        for j in range(1, NT):
             products(j)
         first = fetch(0, *pieces[0])
         for i, piece in enumerate(pieces):

@@ -25,14 +25,16 @@ PAIRS = E // 2
 TB = T // P
 PACK = 4
 GROUPS = E // PACK
-SCALAR_PAIRS = (0, 5)
+SCALAR_PAIRS = (0, 3, 5)
 LAST_CUTS = (0, 512, 768)
-WA_CUTS = (0, 4, 8, 12)
-H_BANKS = 8
+WA_CUTS = (0, 2, 6, 10, 12)
+H_BANKS = 6
+VECTOR_RELUS = (7, 9, 11)
+WA_ROW = 4
 WB_ROW = 8
-TURN_BANK = (2, 4, 5, 0, 1, 6)
-GATE_BANKS = ((1, 2), (7, 4))
-Y_BANKS = ((7, 4, 5, 2), (3, 0, 1), (6, 5, 2), (7, 4, 3))
+TURN_BANK = (6, 7, 0, 4, 3, 5)
+GATE_BANKS = ((6, 7), (3, 4))
+Y_BANKS = ((6, 7, 1, 2), (0, 4, 3), (5, 6, 7), (1, 2, 0))
 Y_CUTS = ((0, 4, 8, 10, 12), (0, 4, 8, 12), (0, 4, 8, 12), (0, 4, 8, 12))
 
 
@@ -55,27 +57,13 @@ def tile_moe_elr_relu_kernel(
 
         xw = keep.tile([P, T], I32, name="xw", align_bytes=64)
         xs = keep.tile([P, T], U8, name="xs", align_bytes=64)
-        wa_sc = [keep.tile([P, H], U8, name="wa_sc%d" % g, align_bytes=64) for g in range(GROUPS)]
-        wy_sc = [keep.tile([P, E, N // 2], U8, name="wy_sc%d" % h, align_bytes=64) for h in range(2)]
+        wy_sc = keep.tile([P, E, N], U8, name="wy_sc", align_bytes=64)
         gate_rows = keep.tile([P, T // 2], F32, name="gate_rows")
         gate_cols = keep.tile([P, TB // 2, 4], F32, name="gate_cols")
         gate_t = [keep.tile([P, T], F32, name="gate_t%d" % r) for r in range(2)]
         ident1 = keep.tile([P, P], F32, name="ident1")
         ident = keep.tile([P, P], F32, name="ident")
         wa_of, w_of, wb_of = {}, {}, {}
-
-        def load_packed(g):
-            for quad in (0, 2, 1, 3):
-                nc.sync.dma_start(
-                    out=wa_sc[g][32 * quad : 32 * quad + 4 * PACK, :].bitcast(I32),
-                    in_=wa_scales[PACK * g : PACK * (g + 1), 0, 4 * quad : 4 * quad + 4, :].bitcast(I32),
-                )
-
-        def load_stepped(row0, scales, half):
-            cols = slice(N // 2 * half, N // 2 * (half + 1))
-            rows = scales[:, 0, :, cols].rearrange("e (q r) n -> r q e n", r=4)
-            for r in range(4):
-                nc.sync.dma_start(out=wy_sc[half][row0 + r : P : 32, :, :].bitcast(I32), in_=rows[r].bitcast(I32))
 
         def load_wa(a, b):
             words = keep.tile([P, b - a, H], I32, name="wa_t%d" % a, align_bytes=64)
@@ -100,42 +88,38 @@ def tile_moe_elr_relu_kernel(
                 w_of.update({(j, e): words[:, e - a, 2 * P * (j - j0) : 2 * P * (j - j0 + 1)] for e in range(a, b)})
 
         nc.gpsimd.memset(xs[:].bitcast(I32), 0)
-        for plane in wa_sc:
-            nc.vector.memset(plane[:].bitcast(I32), 0)
-        for plane in wy_sc:
-            nc.vector.memset(plane[:].rearrange("p e n -> p (e n)").bitcast(I32), 0)
         nc.gpsimd.memset(gate_rows[:], 0.0)
         make_identity(nc, ident1[:])
-        nc.scalar.activation(ident[:], ident1[:], ACT.Relu)
+        nc.vector.memset(wy_sc[:].rearrange("p e n -> p (e n)").bitcast(I32), 0)
 
         nc.sync.dma_start(out=xw[:], in_=x_words[0].rearrange("p t d -> p (t d)").bitcast(I32))
+        nc.sync.dma_start(offs_t[:], offs)
         x_rows = x_scales[0].rearrange("(q r) t -> r q t", r=4)
         for r in range(4):
             nc.sync.dma_start(out=xs[r:P:32, :].bitcast(I32), in_=x_rows[r].bitcast(I32))
-        nc.sync.dma_start(offs_t[:], offs)
         nc.sync.dma_start(out=gate_rows[:4, :], in_=gate[:, 0, :].rearrange("r (h c) -> r h c", h=2))
-        for a, b in spans(WA_CUTS):
+        load_wa(*spans(WA_CUTS)[0])
+        for r in range(4):
+            for row0, scales in ((WA_ROW, wa_scales), (0, w_scales), (WB_ROW, wb_scales)):
+                rows = scales[:, 0].rearrange("e (q r) n -> r q e n", r=4)
+                nc.sync.dma_start(out=wy_sc[row0 + r : P : 32, :, :].bitcast(I32), in_=rows[r].bitcast(I32))
+        nc.scalar.activation(ident[:], ident1[:], ACT.Relu)
+        for a, b in spans(WA_CUTS)[1:]:
             load_wa(a, b)
-            if a % PACK == 0:
-                load_packed(a // PACK)
-        load_w(0, 2, 0, E)
-        load_stepped(0, w_scales, 0)
-        load_wb(0, 0, 4)
-        load_stepped(WB_ROW, wb_scales, 0)
-        load_wb(0, 4, 8)
-        load_wb(0, 8, E)
+        for a, b in spans(Y_CUTS[1]):
+            load_w(0, 2, a, b)
+            for e0, e1 in spans(Y_CUTS[0]):
+                if a <= e0 < b:
+                    load_wb(0, e0, e1)
         for r, pos in enumerate((pos1, pos2)):
             nc.sync.dma_start(pos_t[r][:], pos)
-        load_wb(1, 0, 8)
-        load_wb(1, 8, E)
-        load_stepped(0, w_scales, 1)
-        load_w(2, NT, 0, E)
-        load_stepped(WB_ROW, wb_scales, 1)
-        for j in range(2, NT):
+        for j in range(1, NT):
+            if j == 2:
+                load_w(2, NT, 0, E)
             for a, b in ((0, 8), (8, E)):
                 load_wb(j, a, b)
 
-        turned = psum.tile([P, TB // 2, P], F32, name="bank0")
+        turned = psum.tile([P, TB // 2, P], F32, name="bank5")
         for w in range(TB // 2):
             nc.tensor.transpose(turned[:, w, :], gate_rows[:, P * w : P * (w + 1)], ident[:])
         nc.scalar.copy(gate_cols[:], turned[:, :, :4])
@@ -150,6 +134,7 @@ def tile_moe_elr_relu_kernel(
                 nc.scalar.copy(gate_t[r][:, P * m0 : P * m1], spread[:])
 
         spread_gate(0)
+        spread_gate(1)
 
         gw = keep.tile([P, S], U32, name="gw", align_bytes=64)
         gs = keep.tile([P, S], U8, name="gs", align_bytes=64)
@@ -171,15 +156,16 @@ def tile_moe_elr_relu_kernel(
                     lhsT=gw[:, mine].bitcast(FP8X4),
                     lhsT_scale=gs[:, mine],
                     rhs=wa_of[e].bitcast(FP8X4),
-                    rhs_scale=wa_sc[e // PACK][4 * (e % PACK) : P, :],
+                    rhs_scale=wy_sc[WA_ROW:P, e, :],
                     start=True,
                     stop=True,
                 )
-                nc.scalar.activation(
-                    hb[e][:].rearrange("s (u p d) -> s u p d", u=2, d=2),
-                    hp[:].rearrange("s (p u d) -> s u p d", u=2, d=2),
-                    ACT.Relu,
-                )
+                dst = hb[e][:].rearrange("s (u p d) -> s u p d", u=2, d=2)
+                src = hp[:].rearrange("s (p u d) -> s u p d", u=2, d=2)
+                if e in VECTOR_RELUS:
+                    nc.vector.tensor_scalar_max(dst, src, 0.0)
+                else:
+                    nc.scalar.activation(dst, src, ACT.Relu)
 
         def turn(q):
             tp = psum.tile([P, 2, 2, C], F32, name="bank%d" % TURN_BANK[q])
@@ -200,17 +186,12 @@ def tile_moe_elr_relu_kernel(
 
         for q in range(PAIRS):
             hidden(q)
-        turn(0)
-        for q in range(1, PAIRS):
-            turn(q)
-            quantise(q - 1)
-        quantise(PAIRS - 1)
-
         y = [keep.tile([P, S], F32, name="y%d" % j) for j in range(NT)]
 
-        def products(j):
-            cols = slice(P * (j % 2), P * (j % 2 + 1))
-            for b, (e0, e1) in enumerate(spans(Y_CUTS[j])):
+        def products(j, groups):
+            cols = slice(P * j, P * (j + 1))
+            for b in groups:
+                e0, e1 = spans(Y_CUTS[j])[b]
                 yp = psum.tile([P, (e1 - e0) * C], F32, name="bank%d" % Y_BANKS[j][b])
                 for e in range(e0, e1):
                     a = e - e0
@@ -218,7 +199,7 @@ def tile_moe_elr_relu_kernel(
                     nc.tensor.matmul_mx(
                         out=yp[:, C * a : C * (a + 1)],
                         lhsT=w_of[j, e].bitcast(FP4X4),
-                        lhsT_scale=wy_sc[j // 2][:, e, cols],
+                        lhsT_scale=wy_sc[:, e, cols],
                         rhs=gw[:, mine].bitcast(FP8X4),
                         rhs_scale=gs[:, mine],
                         start=True,
@@ -227,7 +208,7 @@ def tile_moe_elr_relu_kernel(
                     nc.tensor.matmul_mx(
                         out=yp[:, C * a : C * (a + 1)],
                         lhsT=wb_of[j, e].bitcast(FP8X4),
-                        lhsT_scale=wy_sc[j // 2][WB_ROW:P, e, cols],
+                        lhsT_scale=wy_sc[WB_ROW:P, e, cols],
                         rhs=hq[:, mine].bitcast(FP8X4),
                         rhs_scale=hs[:, mine],
                         start=False,
@@ -253,10 +234,14 @@ def tile_moe_elr_relu_kernel(
             nc.vector.tensor_tensor(res[:], both[0][:], both[1][:], ADD)
             nc.sync.dma_start(out=out[P * j : P * (j + 1), t0:t1], in_=res[:])
 
-        products(0)
-        spread_gate(1)
+        turn(0)
+        for q in range(1, PAIRS):
+            turn(q)
+            quantise(q - 1)
+        quantise(PAIRS - 1)
+        products(0, range(GROUPS + 1))
         for j in range(1, NT):
-            products(j)
+            products(j, range(GROUPS))
         first = fetch(0, *pieces[0])
         for i, piece in enumerate(pieces):
             both = [first, fetch(1, *piece)]

@@ -23,19 +23,26 @@ ADD = mybir.AluOpType.add
 NT = N // P
 PAIRS = E // 2
 TB = T // P
-PACK = 4
-GROUPS = E // PACK
-SCALAR_PAIRS = (0, 3, 5)
-LAST_CUTS = (0, 512, 768)
+HALF = TB // 2
+
+W_ROW, WA_ROW, WB_ROW = 0, 4, 8
+
 WA_CUTS = (0, 2, 6, 10, 12)
-H_BANKS = 6
+FIRST_CUTS = (0, 4, 8, 10, 12)
+BANK_CUTS = (0, 4, 8, 12)
+LATE_CUTS = (0, 8, 12)
+LAST_CUTS = (0, 512, 768)
+
 VECTOR_RELUS = (7, 9, 11)
-WA_ROW = 4
-WB_ROW = 8
+SCALAR_TURNS = (0, 3, 5)
+
+H_BANKS = 6
 TURN_BANK = (6, 7, 0, 4, 3, 5)
+GATE_TURN_BANK = 5
 GATE_BANKS = ((6, 7), (3, 4))
 Y_BANKS = ((6, 7, 1, 2), (0, 4, 3), (5, 6, 7), (1, 2, 0))
-Y_CUTS = ((0, 4, 8, 10, 12), (0, 4, 8, 12), (0, 4, 8, 12), (0, 4, 8, 12))
+TURNED_SUMS = (1, 2)
+SUM_BANKS = ((0, 1), (2, 3))
 
 
 def spans(cuts):
@@ -49,7 +56,7 @@ def tile_moe_elr_relu_kernel(
     with ExitStack() as ctx:
         lists = ctx.enter_context(tc.tile_pool(name="lists", bufs=1))
         keep = ctx.enter_context(tc.tile_pool(name="keep", bufs=1))
-        ring = ctx.enter_context(tc.tile_pool(name="ring", bufs=3))
+        ring = ctx.enter_context(tc.tile_pool(name="ring", bufs=NT + 1))
         psum = ctx.enter_context(tc.psum_pool(name="psum", bufs=1))
 
         offs_t = lists.tile([P, S // 16], U16, name="offs_t")
@@ -57,40 +64,41 @@ def tile_moe_elr_relu_kernel(
 
         xw = keep.tile([P, T], I32, name="xw", align_bytes=64)
         xs = keep.tile([P, T], U8, name="xs", align_bytes=64)
-        wy_sc = keep.tile([P, E, N], U8, name="wy_sc", align_bytes=64)
+        planes = keep.tile([P, E, N], U8, name="planes", align_bytes=64)
         gate_rows = keep.tile([P, T // 2], F32, name="gate_rows")
-        gate_cols = keep.tile([P, TB // 2, 4], F32, name="gate_cols")
+        gate_cols = keep.tile([P, HALF, 4], F32, name="gate_cols")
         gate_t = [keep.tile([P, T], F32, name="gate_t%d" % r) for r in range(2)]
-        ident1 = keep.tile([P, P], F32, name="ident1")
+        ident_raw = keep.tile([P, P], F32, name="ident_raw")
         ident = keep.tile([P, P], F32, name="ident")
         wa_of, w_of, wb_of = {}, {}, {}
 
-        def load_wa(a, b):
-            words = keep.tile([P, b - a, H], I32, name="wa_t%d" % a, align_bytes=64)
-            nc.sync.dma_start(out=words[:], in_=wa_words[a:b, 0].rearrange("e p i d -> p e (i d)").bitcast(I32))
-            wa_of.update({e: words[:, e - a, :] for e in range(a, b)})
+        def load_wa(e0, e1):
+            words = keep.tile([P, e1 - e0, H], I32, name="wa_t%d" % e0, align_bytes=64)
+            nc.sync.dma_start(out=words[:], in_=wa_words[e0:e1, 0].rearrange("e p i d -> p e (i d)").bitcast(I32))
+            wa_of.update({e: words[:, e - e0, :] for e in range(e0, e1)})
 
-        def load_wb(j, a, b):
-            words = keep.tile([P, b - a, P], I32, name="wb_t%d_%d" % (j, a), align_bytes=64)
+        def load_wb(j0, j1, e0, e1):
+            words = keep.tile([P, e1 - e0, P * (j1 - j0)], I32, name="wb_t%d_%d" % (j0, e0), align_bytes=64)
             nc.sync.dma_start(
                 out=words[:],
-                in_=wb_words[a:b, 0, :, P * j : P * (j + 1), :].rearrange("e p n d -> p e (n d)").bitcast(I32),
-            )
-            wb_of.update({(j, e): words[:, e - a, :] for e in range(a, b)})
-
-        def load_w(j0, j1, a, b):
-            words = keep.tile([P, b - a, 2 * P * (j1 - j0)], U8, name="w_t%d_%d" % (j0, a), align_bytes=64)
-            nc.sync.dma_start(
-                out=words[:].bitcast(I32),
-                in_=w_words[a:b, 0, :, 2 * P * j0 : 2 * P * j1].rearrange("e p b -> p e b").bitcast(I32),
+                in_=wb_words[e0:e1, 0, :, P * j0 : P * j1, :].rearrange("e p n d -> p e (n d)").bitcast(I32),
             )
             for j in range(j0, j1):
-                w_of.update({(j, e): words[:, e - a, 2 * P * (j - j0) : 2 * P * (j - j0 + 1)] for e in range(a, b)})
+                wb_of.update({(j, e): words[:, e - e0, P * (j - j0) : P * (j - j0 + 1)] for e in range(e0, e1)})
+
+        def load_w(j0, j1, e0, e1):
+            words = keep.tile([P, e1 - e0, 2 * P * (j1 - j0)], U8, name="w_t%d_%d" % (j0, e0), align_bytes=64)
+            nc.sync.dma_start(
+                out=words[:].bitcast(I32),
+                in_=w_words[e0:e1, 0, :, 2 * P * j0 : 2 * P * j1].rearrange("e p b -> p e b").bitcast(I32),
+            )
+            for j in range(j0, j1):
+                w_of.update({(j, e): words[:, e - e0, 2 * P * (j - j0) : 2 * P * (j - j0 + 1)] for e in range(e0, e1)})
 
         nc.gpsimd.memset(xs[:].bitcast(I32), 0)
         nc.gpsimd.memset(gate_rows[:], 0.0)
-        make_identity(nc, ident1[:])
-        nc.vector.memset(wy_sc[:].rearrange("p e n -> p (e n)").bitcast(I32), 0)
+        make_identity(nc, ident_raw[:])
+        nc.vector.memset(planes[:].rearrange("p e n -> p (e n)").bitcast(I32), 0)
 
         nc.sync.dma_start(out=xw[:], in_=x_words[0].rearrange("p t d -> p (t d)").bitcast(I32))
         nc.sync.dma_start(offs_t[:], offs)
@@ -100,41 +108,38 @@ def tile_moe_elr_relu_kernel(
         nc.sync.dma_start(out=gate_rows[:4, :], in_=gate[:, 0, :].rearrange("r (h c) -> r h c", h=2))
         load_wa(*spans(WA_CUTS)[0])
         for r in range(4):
-            for row0, scales in ((WA_ROW, wa_scales), (0, w_scales), (WB_ROW, wb_scales)):
+            for row0, scales in ((WA_ROW, wa_scales), (W_ROW, w_scales), (WB_ROW, wb_scales)):
                 rows = scales[:, 0].rearrange("e (q r) n -> r q e n", r=4)
-                nc.sync.dma_start(out=wy_sc[row0 + r : P : 32, :, :].bitcast(I32), in_=rows[r].bitcast(I32))
-        nc.scalar.activation(ident[:], ident1[:], ACT.Relu)
-        for a, b in spans(WA_CUTS)[1:]:
-            load_wa(a, b)
-        for a, b in spans(Y_CUTS[1]):
-            load_w(0, 2, a, b)
-            for e0, e1 in spans(Y_CUTS[0]):
-                if a <= e0 < b:
-                    load_wb(0, e0, e1)
+                nc.sync.dma_start(out=planes[row0 + r : P : 32, :, :].bitcast(I32), in_=rows[r].bitcast(I32))
+        nc.scalar.activation(ident[:], ident_raw[:], ACT.Relu)
+        for e0, e1 in spans(WA_CUTS)[1:]:
+            load_wa(e0, e1)
+        for g0, g1 in spans(BANK_CUTS):
+            load_w(0, 2, g0, g1)
+            for e0, e1 in spans(FIRST_CUTS):
+                if g0 <= e0 < g1:
+                    load_wb(0, 1, e0, e1)
         for r, pos in enumerate((pos1, pos2)):
             nc.sync.dma_start(pos_t[r][:], pos)
-        for j in range(1, NT):
-            if j == 2:
-                load_w(2, NT, 0, E)
-            for a, b in ((0, 8), (8, E)):
-                load_wb(j, a, b)
+        for e0, e1 in spans(BANK_CUTS):
+            load_wb(1, 3, e0, e1)
+        for e0, e1 in spans(LATE_CUTS):
+            load_w(2, NT, e0, e1)
+        for e0, e1 in spans(LATE_CUTS):
+            load_wb(3, NT, e0, e1)
 
-        turned = psum.tile([P, TB // 2, P], F32, name="bank5")
-        for w in range(TB // 2):
-            nc.tensor.transpose(turned[:, w, :], gate_rows[:, P * w : P * (w + 1)], ident[:])
+        turned = psum.tile([P, HALF, P], F32, name="bank%d" % GATE_TURN_BANK)
+        for m in range(HALF):
+            nc.tensor.transpose(turned[:, m, :], gate_rows[:, P * m : P * (m + 1)], ident[:])
         nc.scalar.copy(gate_cols[:], turned[:, :, :4])
-
-        def spread_gate(r):
+        for r in range(2):
             for bank, (m0, m1) in zip(GATE_BANKS[r], ((0, 4), (4, TB))):
                 spread = psum.tile([P, (m1 - m0) * P], F32, name="bank%d" % bank)
                 for m in range(m0, m1):
-                    row = 2 * r + m // 3
-                    col = gate_cols[:, m % 3, row : row + 1]
+                    row = 2 * r + m // HALF
+                    col = gate_cols[:, m % HALF, row : row + 1]
                     nc.tensor.transpose(spread[:, P * (m - m0) : P * (m - m0 + 1)], col.to_broadcast([P, P]), ident[:])
                 nc.scalar.copy(gate_t[r][:, P * m0 : P * m1], spread[:])
-
-        spread_gate(0)
-        spread_gate(1)
 
         gw = keep.tile([P, S], U32, name="gw", align_bytes=64)
         gs = keep.tile([P, S], U8, name="gs", align_bytes=64)
@@ -143,11 +148,11 @@ def tile_moe_elr_relu_kernel(
         hs = keep.tile([P, S], U8, name="hs", align_bytes=64)
         hg = [keep.tile([P, 2 * C * 4], BF16, name="hg%d" % q, align_bytes=64) for q in range(PAIRS)]
 
-        def hidden(q):
+        for q in range(PAIRS):
             slots = slice(2 * C * q, 2 * C * (q + 1))
-            cols = offs_t[:, 16 * q : 16 * (q + 1)]
-            nc.vector.tensor_copy(gw[:, slots], xw[:].bitcast(U32).indirect(cols))
-            nc.vector.tensor_copy(gs[:, slots], xs[:].indirect(cols))
+            entries = offs_t[:, 2 * C // 16 * q : 2 * C // 16 * (q + 1)]
+            nc.vector.tensor_copy(gw[:, slots], xw[:].bitcast(U32).indirect(entries))
+            nc.vector.tensor_copy(gs[:, slots], xs[:].indirect(entries))
             for e in (2 * q, 2 * q + 1):
                 mine = slice(C * e, C * (e + 1))
                 hp = psum.tile([P, H], F32, name="bank%d" % (e % H_BANKS))
@@ -156,7 +161,7 @@ def tile_moe_elr_relu_kernel(
                     lhsT=gw[:, mine].bitcast(FP8X4),
                     lhsT_scale=gs[:, mine],
                     rhs=wa_of[e].bitcast(FP8X4),
-                    rhs_scale=wy_sc[WA_ROW:P, e, :],
+                    rhs_scale=planes[WA_ROW:P, e, :],
                     start=True,
                     stop=True,
                 )
@@ -166,6 +171,7 @@ def tile_moe_elr_relu_kernel(
                     nc.vector.tensor_scalar_max(dst, src, 0.0)
                 else:
                     nc.scalar.activation(dst, src, ACT.Relu)
+        y = [keep.tile([P, S], F32, name="y%d" % j) for j in range(NT)]
 
         def turn(q):
             tp = psum.tile([P, 2, 2, C], F32, name="bank%d" % TURN_BANK[q])
@@ -175,7 +181,7 @@ def tile_moe_elr_relu_kernel(
                     nc.tensor.transpose(tp[:, a, u, :], words[:, P * u : P * (u + 1)], ident[:])
             dst = hg[q][:].bitcast(F32).rearrange("p (a s u) -> p a s u", a=2, u=2)
             src = tp[:].rearrange("p a u s -> p a s u")
-            if q in SCALAR_PAIRS:
+            if q in SCALAR_TURNS:
                 nc.scalar.copy(dst, src)
             else:
                 nc.vector.tensor_copy(dst, src)
@@ -184,31 +190,26 @@ def tile_moe_elr_relu_kernel(
             slots = slice(2 * C * q, 2 * C * (q + 1))
             nc.vector.quantize_mx(out=hq[:, slots].bitcast(FP8X4), scales=hs[:, slots], in_=hg[q][:])
 
-        for q in range(PAIRS):
-            hidden(q)
-        y = [keep.tile([P, S], F32, name="y%d" % j) for j in range(NT)]
-
-        def products(j, groups):
+        def products(j):
             cols = slice(P * j, P * (j + 1))
-            for b in groups:
-                e0, e1 = spans(Y_CUTS[j])[b]
-                yp = psum.tile([P, (e1 - e0) * C], F32, name="bank%d" % Y_BANKS[j][b])
+            for bank, (e0, e1) in zip(Y_BANKS[j], spans(FIRST_CUTS if j == 0 else BANK_CUTS)):
+                yp = psum.tile([P, (e1 - e0) * C], F32, name="bank%d" % bank)
                 for e in range(e0, e1):
-                    a = e - e0
                     mine = slice(C * e, C * (e + 1))
+                    here = slice(C * (e - e0), C * (e - e0 + 1))
                     nc.tensor.matmul_mx(
-                        out=yp[:, C * a : C * (a + 1)],
+                        out=yp[:, here],
                         lhsT=w_of[j, e].bitcast(FP4X4),
-                        lhsT_scale=wy_sc[:, e, cols],
+                        lhsT_scale=planes[W_ROW:P, e, cols],
                         rhs=gw[:, mine].bitcast(FP8X4),
                         rhs_scale=gs[:, mine],
                         start=True,
                         stop=False,
                     )
                     nc.tensor.matmul_mx(
-                        out=yp[:, C * a : C * (a + 1)],
+                        out=yp[:, here],
                         lhsT=wb_of[j, e].bitcast(FP8X4),
-                        lhsT_scale=wy_sc[WB_ROW:P, e, cols],
+                        lhsT_scale=planes[WB_ROW:P, e, cols],
                         rhs=hq[:, mine].bitcast(FP8X4),
                         rhs_scale=hs[:, mine],
                         start=False,
@@ -219,9 +220,6 @@ def tile_moe_elr_relu_kernel(
                 else:
                     nc.scalar.copy(y[j][:, C * e0 : C * e1], yp[:])
 
-        pieces = [(j, 0, T) for j in range(NT - 1)]
-        pieces += [(NT - 1, a, b) for a, b in spans(LAST_CUTS)]
-
         def fetch(r, j, t0, t1):
             part = ring.tile([P, t1 - t0], F32, name="part%d" % r)
             nc.vector.tensor_tensor(
@@ -229,7 +227,25 @@ def tile_moe_elr_relu_kernel(
             )
             return part
 
-        def finish(j, t0, t1, both):
+        def add_turned(j, both):
+            for half, (bank_sum, bank_back) in enumerate(SUM_BANKS):
+                sums = psum.tile([P, HALF, P], F32, name="bank%d" % bank_sum)
+                for m in range(HALF):
+                    tokens = slice(P * (HALF * half + m), P * (HALF * half + m + 1))
+                    for r in range(2):
+                        nc.tensor.matmul(
+                            sums[:, m, :], both[r][:, tokens], ident[:], start=r == 0, stop=r == 1, is_transpose=True
+                        )
+                mid = ring.tile([P, HALF, P], F32, name="mid")
+                nc.scalar.copy(mid[:], sums[:])
+                back = psum.tile([P, HALF, P], F32, name="bank%d" % bank_back)
+                for m in range(HALF):
+                    nc.tensor.transpose(back[:, m, :], mid[:, m, :], ident[:])
+                done = ring.tile([P, T // 2], F32, name="done")
+                nc.scalar.copy(done[:], back[:].rearrange("p m c -> p (m c)"))
+                nc.scalar.dma_start(out=out[P * j : P * (j + 1), T // 2 * half : T // 2 * (half + 1)], in_=done[:])
+
+        def add(j, t0, t1, both):
             res = ring.tile([P, t1 - t0], F32, name="res")
             nc.vector.tensor_tensor(res[:], both[0][:], both[1][:], ADD)
             nc.sync.dma_start(out=out[P * j : P * (j + 1), t0:t1], in_=res[:])
@@ -239,12 +255,16 @@ def tile_moe_elr_relu_kernel(
             turn(q)
             quantise(q - 1)
         quantise(PAIRS - 1)
-        products(0, range(GROUPS + 1))
-        for j in range(1, NT):
-            products(j, range(GROUPS))
+        for j in range(NT):
+            products(j)
+
+        pieces = [(j, 0, T) for j in range(NT - 1)] + [(NT - 1, t0, t1) for t0, t1 in spans(LAST_CUTS)]
         first = fetch(0, *pieces[0])
-        for i, piece in enumerate(pieces):
+        for n, piece in enumerate(pieces):
             both = [first, fetch(1, *piece)]
-            if i + 1 < len(pieces):
-                first = fetch(0, *pieces[i + 1])
-            finish(*piece, both)
+            if n + 1 < len(pieces):
+                first = fetch(0, *pieces[n + 1])
+            if piece[0] in TURNED_SUMS:
+                add_turned(piece[0], both)
+            else:
+                add(*piece, both)

@@ -31,6 +31,7 @@ WA_CUTS = (0, 2, 6, 10, 12)
 FIRST_CUTS = (0, 4, 8, 10, 12)
 BANK_CUTS = (0, 4, 8, 12)
 LATE_CUTS = (0, 8, 12)
+WB_FIRST_TILE = 2
 LAST_CUTS = (0, 512, 768)
 
 VECTOR_RELUS = (7, 9, 11)
@@ -41,7 +42,7 @@ TURN_BANK = (6, 7, 0, 4, 3, 5)
 GATE_TURN_BANK = 5
 GATE_BANKS = ((6, 7), (3, 4))
 Y_BANKS = ((6, 7, 1, 2), (0, 4, 3), (5, 6, 7), (1, 2, 0))
-TURNED_SUMS = (1, 2)
+TURNED_HALVES = {1: 2, 2: 1}
 SUM_BANKS = ((0, 1), (2, 3))
 
 
@@ -192,29 +193,23 @@ def tile_moe_elr_relu_kernel(
 
         def products(j):
             cols = slice(P * j, P * (j + 1))
+            frozen = (w_of, FP4X4, W_ROW, gw, gs)
+            adapter = (wb_of, FP8X4, WB_ROW, hq, hs)
+            order = (adapter, frozen) if j == WB_FIRST_TILE else (frozen, adapter)
             for bank, (e0, e1) in zip(Y_BANKS[j], spans(FIRST_CUTS if j == 0 else BANK_CUTS)):
                 yp = psum.tile([P, (e1 - e0) * C], F32, name="bank%d" % bank)
-                for e in range(e0, e1):
-                    mine = slice(C * e, C * (e + 1))
-                    here = slice(C * (e - e0), C * (e - e0 + 1))
-                    nc.tensor.matmul_mx(
-                        out=yp[:, here],
-                        lhsT=w_of[j, e].bitcast(FP4X4),
-                        lhsT_scale=planes[W_ROW:P, e, cols],
-                        rhs=gw[:, mine].bitcast(FP8X4),
-                        rhs_scale=gs[:, mine],
-                        start=True,
-                        stop=False,
-                    )
-                    nc.tensor.matmul_mx(
-                        out=yp[:, here],
-                        lhsT=wb_of[j, e].bitcast(FP8X4),
-                        lhsT_scale=planes[WB_ROW:P, e, cols],
-                        rhs=hq[:, mine].bitcast(FP8X4),
-                        rhs_scale=hs[:, mine],
-                        start=False,
-                        stop=True,
-                    )
+                for n, (weights, dtype, row0, words, scales) in enumerate(order):
+                    for e in range(e0, e1):
+                        mine = slice(C * e, C * (e + 1))
+                        nc.tensor.matmul_mx(
+                            out=yp[:, C * (e - e0) : C * (e - e0 + 1)],
+                            lhsT=weights[j, e].bitcast(dtype),
+                            lhsT_scale=planes[row0:P, e, cols],
+                            rhs=words[:, mine].bitcast(FP8X4),
+                            rhs_scale=scales[:, mine],
+                            start=n == 0 and e == e0,
+                            stop=n == 1 and e == e1 - 1,
+                        )
                 if j == 0 and e1 == E:
                     nc.vector.tensor_copy(y[j][:, C * e0 : C * e1], yp[:])
                 else:
@@ -228,7 +223,7 @@ def tile_moe_elr_relu_kernel(
             return part
 
         def add_turned(j, both):
-            for half, (bank_sum, bank_back) in enumerate(SUM_BANKS):
+            for half, (bank_sum, bank_back) in enumerate(SUM_BANKS[: TURNED_HALVES[j]]):
                 sums = psum.tile([P, HALF, P], F32, name="bank%d" % bank_sum)
                 for m in range(HALF):
                     tokens = slice(P * (HALF * half + m), P * (HALF * half + m + 1))
@@ -245,10 +240,10 @@ def tile_moe_elr_relu_kernel(
                 nc.scalar.copy(done[:], back[:].rearrange("p m c -> p (m c)"))
                 nc.scalar.dma_start(out=out[P * j : P * (j + 1), T // 2 * half : T // 2 * (half + 1)], in_=done[:])
 
-        def add(j, t0, t1, both):
-            res = ring.tile([P, t1 - t0], F32, name="res")
-            nc.vector.tensor_tensor(res[:], both[0][:], both[1][:], ADD)
-            nc.sync.dma_start(out=out[P * j : P * (j + 1), t0:t1], in_=res[:])
+        def add(j, t0, t1, both, skip):
+            res = ring.tile([P, t1 - t0 - skip], F32, name="res")
+            nc.vector.tensor_tensor(res[:], both[0][:, skip:], both[1][:, skip:], ADD)
+            nc.sync.dma_start(out=out[P * j : P * (j + 1), t0 + skip : t1], in_=res[:])
 
         turn(0)
         for q in range(1, PAIRS):
@@ -264,7 +259,8 @@ def tile_moe_elr_relu_kernel(
             both = [first, fetch(1, *piece)]
             if n + 1 < len(pieces):
                 first = fetch(0, *pieces[n + 1])
-            if piece[0] in TURNED_SUMS:
+            halves = TURNED_HALVES.get(piece[0], 0)
+            if halves:
                 add_turned(piece[0], both)
-            else:
-                add(*piece, both)
+            if halves < 2:
+                add(*piece, both, halves * T // 2)

@@ -42,7 +42,7 @@ TURN_BANK = (6, 7, 0, 4, 3, 5)
 GATE_TURN_BANK = 5
 GATE_BANKS = ((6, 7), (3, 4))
 Y_BANKS = ((6, 7, 1, 2), (0, 4, 3), (5, 6, 7), (1, 2, 0))
-TURNED_HALVES = {1: 2, 2: 1}
+TURNED_HALVES = {1: 2, 2: 2}
 SUM_BANKS = ((0, 1), (2, 3))
 
 

@@ -25,6 +25,8 @@ PAIRS = E // 2
 TB = T // P
 HALF = TB // 2
 
+ALIGN = 256
+
 W_ROW, WA_ROW, WB_ROW = 0, 4, 8
 
 WA_CUTS = (0, 2, 6, 10, 12)
@@ -63,10 +65,10 @@ def tile_moe_elr_relu_kernel(
         offs_t = lists.tile([P, S // 16], U16, name="offs_t")
         pos_t = [lists.tile([P, T // 16], U16, name="pos%d_t" % r) for r in (1, 2)]
 
-        xw = keep.tile([P, T], I32, name="xw", align_bytes=64)
-        xs = keep.tile([P, T], U8, name="xs", align_bytes=64)
-        planes = keep.tile([P, E, N], U8, name="planes", align_bytes=64)
-        gate_rows = keep.tile([P, T // 2], F32, name="gate_rows")
+        xw = keep.tile([P, T], I32, name="xw", align_bytes=ALIGN)
+        xs = keep.tile([P, T], U8, name="xs", align_bytes=ALIGN)
+        planes = keep.tile([P, E, N], U8, name="planes", align_bytes=ALIGN)
+        gate_rows = keep.tile([P, T // 2], F32, name="gate_rows", align_bytes=ALIGN)
         gate_cols = keep.tile([P, HALF, 4], F32, name="gate_cols")
         gate_t = [keep.tile([P, T], F32, name="gate_t%d" % r) for r in range(2)]
         ident_raw = keep.tile([P, P], F32, name="ident_raw")
@@ -74,12 +76,12 @@ def tile_moe_elr_relu_kernel(
         wa_of, w_of, wb_of = {}, {}, {}
 
         def load_wa(e0, e1):
-            words = keep.tile([P, e1 - e0, H], I32, name="wa_t%d" % e0, align_bytes=64)
+            words = keep.tile([P, e1 - e0, H], I32, name="wa_t%d" % e0, align_bytes=ALIGN)
             nc.sync.dma_start(out=words[:], in_=wa_words[e0:e1, 0].rearrange("e p i d -> p e (i d)").bitcast(I32))
             wa_of.update({e: words[:, e - e0, :] for e in range(e0, e1)})
 
         def load_wb(j0, j1, e0, e1):
-            words = keep.tile([P, e1 - e0, P * (j1 - j0)], I32, name="wb_t%d_%d" % (j0, e0), align_bytes=64)
+            words = keep.tile([P, e1 - e0, P * (j1 - j0)], I32, name="wb_t%d_%d" % (j0, e0), align_bytes=ALIGN)
             nc.sync.dma_start(
                 out=words[:],
                 in_=wb_words[e0:e1, 0, :, P * j0 : P * j1, :].rearrange("e p n d -> p e (n d)").bitcast(I32),
@@ -88,7 +90,7 @@ def tile_moe_elr_relu_kernel(
                 wb_of.update({(j, e): words[:, e - e0, P * (j - j0) : P * (j - j0 + 1)] for e in range(e0, e1)})
 
         def load_w(j0, j1, e0, e1):
-            words = keep.tile([P, e1 - e0, 2 * P * (j1 - j0)], U8, name="w_t%d_%d" % (j0, e0), align_bytes=64)
+            words = keep.tile([P, e1 - e0, 2 * P * (j1 - j0)], U8, name="w_t%d_%d" % (j0, e0), align_bytes=ALIGN)
             nc.sync.dma_start(
                 out=words[:].bitcast(I32),
                 in_=w_words[e0:e1, 0, :, 2 * P * j0 : 2 * P * j1].rearrange("e p b -> p e b").bitcast(I32),
@@ -122,7 +124,7 @@ def tile_moe_elr_relu_kernel(
                     load_wb(0, 1, e0, e1)
         for r, pos in enumerate((pos1, pos2)):
             nc.sync.dma_start(pos_t[r][:], pos)
-        for e0, e1 in spans(BANK_CUTS):
+        for e0, e1 in spans(FIRST_CUTS):
             load_wb(1, 3, e0, e1)
         for e0, e1 in spans(LATE_CUTS):
             load_w(2, NT, e0, e1)
@@ -142,12 +144,12 @@ def tile_moe_elr_relu_kernel(
                     nc.tensor.transpose(spread[:, P * (m - m0) : P * (m - m0 + 1)], col.to_broadcast([P, P]), ident[:])
                 nc.scalar.copy(gate_t[r][:, P * m0 : P * m1], spread[:])
 
-        gw = keep.tile([P, S], U32, name="gw", align_bytes=64)
-        gs = keep.tile([P, S], U8, name="gs", align_bytes=64)
-        hb = [keep.tile([P, H], BF16, name="hb%d" % e, align_bytes=64) for e in range(E)]
-        hq = keep.tile([P, S], U32, name="hq", align_bytes=64)
-        hs = keep.tile([P, S], U8, name="hs", align_bytes=64)
-        hg = [keep.tile([P, 2 * C * 4], BF16, name="hg%d" % q, align_bytes=64) for q in range(PAIRS)]
+        gw = keep.tile([P, S], U32, name="gw", align_bytes=ALIGN)
+        gs = keep.tile([P, S], U8, name="gs", align_bytes=ALIGN)
+        hb = [keep.tile([P, H], BF16, name="hb%d" % e, align_bytes=ALIGN) for e in range(E)]
+        hq = keep.tile([P, S], U32, name="hq", align_bytes=ALIGN)
+        hs = keep.tile([P, S], U8, name="hs", align_bytes=ALIGN)
+        hg = [keep.tile([P, 2 * C * 4], BF16, name="hg%d" % q, align_bytes=ALIGN) for q in range(PAIRS)]
 
         for q in range(PAIRS):
             slots = slice(2 * C * q, 2 * C * (q + 1))
@@ -236,12 +238,12 @@ def tile_moe_elr_relu_kernel(
                 back = psum.tile([P, HALF, P], F32, name="bank%d" % bank_back)
                 for m in range(HALF):
                     nc.tensor.transpose(back[:, m, :], mid[:, m, :], ident[:])
-                done = ring.tile([P, T // 2], F32, name="done")
+                done = ring.tile([P, T // 2], F32, name="done", align_bytes=ALIGN)
                 nc.scalar.copy(done[:], back[:].rearrange("p m c -> p (m c)"))
                 nc.scalar.dma_start(out=out[P * j : P * (j + 1), T // 2 * half : T // 2 * (half + 1)], in_=done[:])
 
         def add(j, t0, t1, both, skip):
-            res = ring.tile([P, t1 - t0 - skip], F32, name="res")
+            res = ring.tile([P, t1 - t0 - skip], F32, name="res", align_bytes=ALIGN)
             nc.vector.tensor_tensor(res[:], both[0][:, skip:], both[1][:, skip:], ADD)
             nc.sync.dma_start(out=out[P * j : P * (j + 1), t0 + skip : t1], in_=res[:])
 

@@ -29,12 +29,12 @@ ALIGN = 256
 
 W_ROW, WA_ROW, WB_ROW = 0, 4, 8
 
-WA_CUTS = (0, 2, 6, 10, 12)
-FIRST_CUTS = (0, 4, 8, 10, 12)
+WA_CUTS = (0, 3, 6, 10, 12)
 BANK_CUTS = (0, 4, 8, 12)
+FINE_CUTS = (0, 4, 8, 10, 12)
 LATE_CUTS = (0, 8, 12)
 WB_FIRST_TILE = 2
-LAST_CUTS = (0, 512, 768)
+LAST_CUTS = (0, 448, 640, 768)
 
 VECTOR_RELUS = (7, 9, 11)
 SCALAR_TURNS = (0, 3, 5)
@@ -44,8 +44,7 @@ TURN_BANK = (6, 7, 0, 4, 3, 5)
 GATE_TURN_BANK = 5
 GATE_BANKS = ((6, 7), (3, 4))
 Y_BANKS = ((6, 7, 1, 2), (0, 4, 3), (5, 6, 7), (1, 2, 0))
-TURNED_HALVES = {1: 2, 2: 2}
-SUM_BANKS = ((0, 1), (2, 3))
+SUM_BANKS = {1: ((3, 4), (5, 6)), 2: ((5, 3), (4, 6))}
 
 
 def spans(cuts):
@@ -59,7 +58,7 @@ def tile_moe_elr_relu_kernel(
     with ExitStack() as ctx:
         lists = ctx.enter_context(tc.tile_pool(name="lists", bufs=1))
         keep = ctx.enter_context(tc.tile_pool(name="keep", bufs=1))
-        ring = ctx.enter_context(tc.tile_pool(name="ring", bufs=NT + 1))
+        ring = ctx.enter_context(tc.tile_pool(name="ring", bufs=NT + 2))
         psum = ctx.enter_context(tc.psum_pool(name="psum", bufs=1))
 
         offs_t = lists.tile([P, S // 16], U16, name="offs_t")
@@ -119,12 +118,12 @@ def tile_moe_elr_relu_kernel(
             load_wa(e0, e1)
         for g0, g1 in spans(BANK_CUTS):
             load_w(0, 2, g0, g1)
-            for e0, e1 in spans(FIRST_CUTS):
+            for e0, e1 in spans(FINE_CUTS):
                 if g0 <= e0 < g1:
                     load_wb(0, 1, e0, e1)
         for r, pos in enumerate((pos1, pos2)):
             nc.sync.dma_start(pos_t[r][:], pos)
-        for e0, e1 in spans(FIRST_CUTS):
+        for e0, e1 in spans(FINE_CUTS):
             load_wb(1, 3, e0, e1)
         for e0, e1 in spans(LATE_CUTS):
             load_w(2, NT, e0, e1)
@@ -198,7 +197,7 @@ def tile_moe_elr_relu_kernel(
             frozen = (w_of, FP4X4, W_ROW, gw, gs)
             adapter = (wb_of, FP8X4, WB_ROW, hq, hs)
             order = (adapter, frozen) if j == WB_FIRST_TILE else (frozen, adapter)
-            for bank, (e0, e1) in zip(Y_BANKS[j], spans(FIRST_CUTS if j == 0 else BANK_CUTS)):
+            for bank, (e0, e1) in zip(Y_BANKS[j], spans(FINE_CUTS if j == 0 else BANK_CUTS)):
                 yp = psum.tile([P, (e1 - e0) * C], F32, name="bank%d" % bank)
                 for n, (weights, dtype, row0, words, scales) in enumerate(order):
                     for e in range(e0, e1):
@@ -225,7 +224,7 @@ def tile_moe_elr_relu_kernel(
             return part
 
         def add_turned(j, both):
-            for half, (bank_sum, bank_back) in enumerate(SUM_BANKS[: TURNED_HALVES[j]]):
+            for half, (bank_sum, bank_back) in enumerate(SUM_BANKS[j]):
                 sums = psum.tile([P, HALF, P], F32, name="bank%d" % bank_sum)
                 for m in range(HALF):
                     tokens = slice(P * (HALF * half + m), P * (HALF * half + m + 1))
@@ -242,10 +241,10 @@ def tile_moe_elr_relu_kernel(
                 nc.scalar.copy(done[:], back[:].rearrange("p m c -> p (m c)"))
                 nc.scalar.dma_start(out=out[P * j : P * (j + 1), T // 2 * half : T // 2 * (half + 1)], in_=done[:])
 
-        def add(j, t0, t1, both, skip):
-            res = ring.tile([P, t1 - t0 - skip], F32, name="res", align_bytes=ALIGN)
-            nc.vector.tensor_tensor(res[:], both[0][:, skip:], both[1][:, skip:], ADD)
-            nc.sync.dma_start(out=out[P * j : P * (j + 1), t0 + skip : t1], in_=res[:])
+        def add(j, t0, t1, both):
+            res = ring.tile([P, t1 - t0], F32, name="res", align_bytes=ALIGN)
+            nc.vector.tensor_tensor(res[:], both[0][:], both[1][:], ADD)
+            nc.sync.dma_start(out=out[P * j : P * (j + 1), t0:t1], in_=res[:])
 
         turn(0)
         for q in range(1, PAIRS):
@@ -256,13 +255,14 @@ def tile_moe_elr_relu_kernel(
             products(j)
 
         pieces = [(j, 0, T) for j in range(NT - 1)] + [(NT - 1, t0, t1) for t0, t1 in spans(LAST_CUTS)]
-        first = fetch(0, *pieces[0])
-        for n, piece in enumerate(pieces):
-            both = [first, fetch(1, *piece)]
-            if n + 1 < len(pieces):
-                first = fetch(0, *pieces[n + 1])
-            halves = TURNED_HALVES.get(piece[0], 0)
-            if halves:
-                add_turned(piece[0], both)
-            if halves < 2:
-                add(*piece, both, halves * T // 2)
+        parts = [[fetch(0, *pieces[0])]]
+        for n, piece in enumerate(pieces[:-1]):
+            parts[n].append(fetch(1, *piece))
+            parts.append([fetch(0, *pieces[n + 1])])
+            if piece[0] in SUM_BANKS:
+                add_turned(piece[0], parts[n])
+            elif n < len(pieces) - 2:
+                add(*piece, parts[n])
+        parts[-1].append(fetch(1, *pieces[-1]))
+        for piece, both in zip(pieces[-2:], parts[-2:]):
+            add(*piece, both)

@@ -33,8 +33,7 @@ WA_CUTS = (0, 3, 6, 10, 12)
 BANK_CUTS = (0, 4, 8, 12)
 FINE_CUTS = (0, 4, 8, 10, 12)
 LATE_CUTS = (0, 8, 12)
-WB_FIRST_TILE = 2
-LAST_CUTS = (0, 448, 640, 768)
+LAST_CUTS = (0, 512, 768)
 
 VECTOR_RELUS = (7, 9, 11)
 SCALAR_TURNS = (0, 3, 5)
@@ -44,7 +43,6 @@ TURN_BANK = (6, 7, 0, 4, 3, 5)
 GATE_TURN_BANK = 5
 GATE_BANKS = ((6, 7), (3, 4))
 Y_BANKS = ((6, 7, 1, 2), (0, 4, 3), (5, 6, 7), (1, 2, 0))
-SUM_BANKS = {1: ((3, 4), (5, 6)), 2: ((5, 3), (4, 6))}
 
 
 def spans(cuts):
@@ -58,7 +56,7 @@ def tile_moe_elr_relu_kernel(
     with ExitStack() as ctx:
         lists = ctx.enter_context(tc.tile_pool(name="lists", bufs=1))
         keep = ctx.enter_context(tc.tile_pool(name="keep", bufs=1))
-        ring = ctx.enter_context(tc.tile_pool(name="ring", bufs=NT + 2))
+        ring = ctx.enter_context(tc.tile_pool(name="ring", bufs=NT + 1))
         psum = ctx.enter_context(tc.psum_pool(name="psum", bufs=1))
 
         offs_t = lists.tile([P, S // 16], U16, name="offs_t")
@@ -123,10 +121,11 @@ def tile_moe_elr_relu_kernel(
                     load_wb(0, 1, e0, e1)
         for r, pos in enumerate((pos1, pos2)):
             nc.sync.dma_start(pos_t[r][:], pos)
-        for e0, e1 in spans(FINE_CUTS):
-            load_wb(1, 3, e0, e1)
+        for e0, e1 in spans(LATE_CUTS):
+            load_wb(1, 2, e0, e1)
         for e0, e1 in spans(LATE_CUTS):
             load_w(2, NT, e0, e1)
+            load_wb(2, 3, e0, e1)
         for e0, e1 in spans(LATE_CUTS):
             load_wb(3, NT, e0, e1)
 
@@ -173,7 +172,6 @@ def tile_moe_elr_relu_kernel(
                     nc.vector.tensor_scalar_max(dst, src, 0.0)
                 else:
                     nc.scalar.activation(dst, src, ACT.Relu)
-        y = [keep.tile([P, S], F32, name="y%d" % j) for j in range(NT)]
 
         def turn(q):
             tp = psum.tile([P, 2, 2, C], F32, name="bank%d" % TURN_BANK[q])
@@ -193,13 +191,13 @@ def tile_moe_elr_relu_kernel(
             nc.vector.quantize_mx(out=hq[:, slots].bitcast(FP8X4), scales=hs[:, slots], in_=hg[q][:])
 
         def products(j):
+            y = keep.tile([P, S], F32, name="y%d" % j)
             cols = slice(P * j, P * (j + 1))
             frozen = (w_of, FP4X4, W_ROW, gw, gs)
             adapter = (wb_of, FP8X4, WB_ROW, hq, hs)
-            order = (adapter, frozen) if j == WB_FIRST_TILE else (frozen, adapter)
             for bank, (e0, e1) in zip(Y_BANKS[j], spans(FINE_CUTS if j == 0 else BANK_CUTS)):
                 yp = psum.tile([P, (e1 - e0) * C], F32, name="bank%d" % bank)
-                for n, (weights, dtype, row0, words, scales) in enumerate(order):
+                for n, (weights, dtype, row0, words, scales) in enumerate((frozen, adapter)):
                     for e in range(e0, e1):
                         mine = slice(C * e, C * (e + 1))
                         nc.tensor.matmul_mx(
@@ -212,57 +210,40 @@ def tile_moe_elr_relu_kernel(
                             stop=n == 1 and e == e1 - 1,
                         )
                 if j == 0 and e1 == E:
-                    nc.vector.tensor_copy(y[j][:, C * e0 : C * e1], yp[:])
+                    nc.vector.tensor_copy(y[:, C * e0 : C * e1], yp[:])
                 else:
-                    nc.scalar.copy(y[j][:, C * e0 : C * e1], yp[:])
+                    nc.scalar.copy(y[:, C * e0 : C * e1], yp[:])
+            return y
 
-        def fetch(r, j, t0, t1):
-            part = ring.tile([P, t1 - t0], F32, name="part%d" % r)
-            nc.vector.tensor_tensor(
-                part[:], y[j][:].indirect(pos_t[r][:, t0 // 16 : t1 // 16]), gate_t[r][:, t0:t1], MULT
-            )
-            return part
+        def fetch(y):
+            second = ring.tile([P, T], F32, name="second")
+            nc.scalar.activation(second[:], y[:].indirect(pos_t[1][:]), ACT.Copy)
+            first = ring.tile([P, T], F32, name="first")
+            nc.vector.tensor_tensor(first[:], y[:].indirect(pos_t[0][:]), gate_t[0][:], MULT)
+            return first, second
 
-        def add_turned(j, both):
-            for half, (bank_sum, bank_back) in enumerate(SUM_BANKS[j]):
-                sums = psum.tile([P, HALF, P], F32, name="bank%d" % bank_sum)
-                for m in range(HALF):
-                    tokens = slice(P * (HALF * half + m), P * (HALF * half + m + 1))
-                    for r in range(2):
-                        nc.tensor.matmul(
-                            sums[:, m, :], both[r][:, tokens], ident[:], start=r == 0, stop=r == 1, is_transpose=True
-                        )
-                mid = ring.tile([P, HALF, P], F32, name="mid")
-                nc.scalar.copy(mid[:], sums[:])
-                back = psum.tile([P, HALF, P], F32, name="bank%d" % bank_back)
-                for m in range(HALF):
-                    nc.tensor.transpose(back[:, m, :], mid[:, m, :], ident[:])
-                done = ring.tile([P, T // 2], F32, name="done", align_bytes=ALIGN)
-                nc.scalar.copy(done[:], back[:].rearrange("p m c -> p (m c)"))
-                nc.scalar.dma_start(out=out[P * j : P * (j + 1), T // 2 * half : T // 2 * (half + 1)], in_=done[:])
+        def weigh(second, cuts):
+            gated = ring.tile([P, T], F32, name="gated")
+            for t0, t1 in spans(cuts):
+                nc.vector.tensor_tensor(gated[:, t0:t1], second[:, t0:t1], gate_t[1][:, t0:t1], MULT)
+            return gated
 
-        def add(j, t0, t1, both):
-            res = ring.tile([P, t1 - t0], F32, name="res", align_bytes=ALIGN)
-            nc.vector.tensor_tensor(res[:], both[0][:], both[1][:], ADD)
-            nc.sync.dma_start(out=out[P * j : P * (j + 1), t0:t1], in_=res[:])
+        def add(j, first, gated, cuts):
+            for t0, t1 in spans(cuts):
+                res = ring.tile([P, t1 - t0], F32, name="res", align_bytes=ALIGN)
+                nc.vector.tensor_tensor(res[:], first[:, t0:t1], gated[:, t0:t1], ADD)
+                nc.sync.dma_start(out=out[P * j : P * (j + 1), t0:t1], in_=res[:])
 
         turn(0)
         for q in range(1, PAIRS):
             turn(q)
             quantise(q - 1)
         quantise(PAIRS - 1)
+        waiting = []
         for j in range(NT):
-            products(j)
-
-        pieces = [(j, 0, T) for j in range(NT - 1)] + [(NT - 1, t0, t1) for t0, t1 in spans(LAST_CUTS)]
-        parts = [[fetch(0, *pieces[0])]]
-        for n, piece in enumerate(pieces[:-1]):
-            parts[n].append(fetch(1, *piece))
-            parts.append([fetch(0, *pieces[n + 1])])
-            if piece[0] in SUM_BANKS:
-                add_turned(piece[0], parts[n])
-            elif n < len(pieces) - 2:
-                add(*piece, parts[n])
-        parts[-1].append(fetch(1, *pieces[-1]))
-        for piece, both in zip(pieces[-2:], parts[-2:]):
-            add(*piece, both)
+            first, second = fetch(products(j))
+            for args in waiting:
+                add(*args)
+            cuts = LAST_CUTS if j == NT - 1 else (0, T)
+            waiting = [(j, first, weigh(second, cuts), cuts)]
+        add(*waiting[0])

@@ -29,20 +29,20 @@ ALIGN = 256
 
 W_ROW, WA_ROW, WB_ROW = 0, 4, 8
 
-WA_CUTS = (0, 3, 6, 10, 12)
+WA_CUTS = (0, 4, 8, 10, 12)
 BANK_CUTS = (0, 4, 8, 12)
 FINE_CUTS = (0, 4, 8, 10, 12)
 LATE_CUTS = (0, 8, 12)
 LAST_CUTS = (0, 512, 768)
 
-VECTOR_RELUS = (7, 9, 11)
-SCALAR_TURNS = (0, 3, 5)
+VECTOR_RELUS = (5, 7, 9, 11)
+SCALAR_TURNS = (0, 1, 2, 3, 4, 5)
 
 H_BANKS = 6
-TURN_BANK = (6, 7, 0, 4, 3, 5)
-GATE_TURN_BANK = 5
-GATE_BANKS = ((6, 7), (3, 4))
-Y_BANKS = ((6, 7, 1, 2), (0, 4, 3), (5, 6, 7), (1, 2, 0))
+AHEAD = 2
+TURN_BANK = (6, 7, 6, 7, 6, 7)
+GATE_BANKS = ((4, 5), (6, 7))
+Y_BANKS = ((0, 1, 2, 3), (4, 5, 6), (7, 0, 1), (2, 3, 4))
 
 
 def spans(cuts):
@@ -65,8 +65,8 @@ def tile_moe_elr_relu_kernel(
         xw = keep.tile([P, T], I32, name="xw", align_bytes=ALIGN)
         xs = keep.tile([P, T], U8, name="xs", align_bytes=ALIGN)
         planes = keep.tile([P, E, N], U8, name="planes", align_bytes=ALIGN)
-        gate_rows = keep.tile([P, T // 2], F32, name="gate_rows", align_bytes=ALIGN)
-        gate_cols = keep.tile([P, HALF, 4], F32, name="gate_cols")
+        wa_plane = keep.tile([P, E, H], U8, name="wa_plane", align_bytes=ALIGN)
+        gate_cols = keep.tile([P, 2, 2, 8], F32, name="gate_cols")
         gate_t = [keep.tile([P, T], F32, name="gate_t%d" % r) for r in range(2)]
         ident_raw = keep.tile([P, P], F32, name="ident_raw")
         ident = keep.tile([P, P], F32, name="ident")
@@ -95,22 +95,25 @@ def tile_moe_elr_relu_kernel(
             for j in range(j0, j1):
                 w_of.update({(j, e): words[:, e - e0, 2 * P * (j - j0) : 2 * P * (j - j0 + 1)] for e in range(e0, e1)})
 
+        def load_gate(r):
+            nc.sync.dma_start(out=gate_cols[:, r, :, :HALF], in_=gate[r, 0, :].rearrange("(h p c) -> p h c", h=2, c=HALF))
+
         nc.gpsimd.memset(xs[:].bitcast(I32), 0)
-        nc.gpsimd.memset(gate_rows[:], 0.0)
         make_identity(nc, ident_raw[:])
-        nc.vector.memset(planes[:].rearrange("p e n -> p (e n)").bitcast(I32), 0)
 
         nc.sync.dma_start(out=xw[:], in_=x_words[0].rearrange("p t d -> p (t d)").bitcast(I32))
         nc.sync.dma_start(offs_t[:], offs)
+        load_gate(0)
         x_rows = x_scales[0].rearrange("(q r) t -> r q t", r=4)
         for r in range(4):
             nc.sync.dma_start(out=xs[r:P:32, :].bitcast(I32), in_=x_rows[r].bitcast(I32))
-        nc.sync.dma_start(out=gate_rows[:4, :], in_=gate[:, 0, :].rearrange("r (h c) -> r h c", h=2))
         load_wa(*spans(WA_CUTS)[0])
-        for r in range(4):
-            for row0, scales in ((WA_ROW, wa_scales), (W_ROW, w_scales), (WB_ROW, wb_scales)):
-                rows = scales[:, 0].rearrange("e (q r) n -> r q e n", r=4)
-                nc.sync.dma_start(out=planes[row0 + r : P : 32, :, :].bitcast(I32), in_=rows[r].bitcast(I32))
+        load_gate(1)
+        others = [(planes, row0, scales, r) for r in range(4) for row0, scales in ((W_ROW, w_scales), (WB_ROW, wb_scales))]
+        run = [load for r in range(4) for load in ((wa_plane, WA_ROW, wa_scales, r), others[r])] + others[4:]
+        for tile, row0, scales, r in run:
+            rows = scales[:, 0].rearrange("e (q r) n -> r q e n", r=4)
+            nc.sync.dma_start(out=tile[row0 + r : P : 32, :, :].bitcast(I32), in_=rows[r].bitcast(I32))
         nc.scalar.activation(ident[:], ident_raw[:], ACT.Relu)
         for e0, e1 in spans(WA_CUTS)[1:]:
             load_wa(e0, e1)
@@ -129,18 +132,13 @@ def tile_moe_elr_relu_kernel(
         for e0, e1 in spans(LATE_CUTS):
             load_wb(3, NT, e0, e1)
 
-        turned = psum.tile([P, HALF, P], F32, name="bank%d" % GATE_TURN_BANK)
-        for m in range(HALF):
-            nc.tensor.transpose(turned[:, m, :], gate_rows[:, P * m : P * (m + 1)], ident[:])
-        nc.scalar.copy(gate_cols[:], turned[:, :, :4])
         for r in range(2):
-            for bank, (m0, m1) in zip(GATE_BANKS[r], ((0, 4), (4, TB))):
-                spread = psum.tile([P, (m1 - m0) * P], F32, name="bank%d" % bank)
-                for m in range(m0, m1):
-                    row = 2 * r + m // HALF
-                    col = gate_cols[:, m % HALF, row : row + 1]
-                    nc.tensor.transpose(spread[:, P * (m - m0) : P * (m - m0 + 1)], col.to_broadcast([P, P]), ident[:])
-                nc.scalar.copy(gate_t[r][:, P * m0 : P * m1], spread[:])
+            for h, bank in enumerate(GATE_BANKS[r]):
+                spread = psum.tile([P, HALF, P], F32, name="bank%d" % bank)
+                for c in range(HALF):
+                    nc.tensor.transpose(spread[:, c, :], gate_cols[:, r, h, c : c + 1].to_broadcast([P, P]), ident[:])
+                half = gate_t[r][:, T // 2 * h : T // 2 * (h + 1)]
+                nc.scalar.copy(half.rearrange("p (n c) -> p n c", c=HALF), spread[:].rearrange("p c n -> p n c"))
 
         gw = keep.tile([P, S], U32, name="gw", align_bytes=ALIGN)
         gs = keep.tile([P, S], U8, name="gs", align_bytes=ALIGN)
@@ -154,6 +152,8 @@ def tile_moe_elr_relu_kernel(
             entries = offs_t[:, 2 * C // 16 * q : 2 * C // 16 * (q + 1)]
             nc.vector.tensor_copy(gw[:, slots], xw[:].bitcast(U32).indirect(entries))
             nc.vector.tensor_copy(gs[:, slots], xs[:].indirect(entries))
+
+        def hidden(q):
             for e in (2 * q, 2 * q + 1):
                 mine = slice(C * e, C * (e + 1))
                 hp = psum.tile([P, H], F32, name="bank%d" % (e % H_BANKS))
@@ -162,7 +162,7 @@ def tile_moe_elr_relu_kernel(
                     lhsT=gw[:, mine].bitcast(FP8X4),
                     lhsT_scale=gs[:, mine],
                     rhs=wa_of[e].bitcast(FP8X4),
-                    rhs_scale=planes[WA_ROW:P, e, :],
+                    rhs_scale=wa_plane[WA_ROW:P, e, :],
                     start=True,
                     stop=True,
                 )
@@ -234,10 +234,14 @@ def tile_moe_elr_relu_kernel(
                 nc.vector.tensor_tensor(res[:], first[:, t0:t1], gated[:, t0:t1], ADD)
                 nc.sync.dma_start(out=out[P * j : P * (j + 1), t0:t1], in_=res[:])
 
-        turn(0)
-        for q in range(1, PAIRS):
+        for q in range(AHEAD):
+            hidden(q)
+        for q in range(PAIRS):
+            if q + AHEAD < PAIRS:
+                hidden(q + AHEAD)
             turn(q)
-            quantise(q - 1)
+            if q > 0:
+                quantise(q - 1)
         quantise(PAIRS - 1)
         waiting = []
         for j in range(NT):

@@ -29,20 +29,20 @@ ALIGN = 256
 
 W_ROW, WA_ROW, WB_ROW = 0, 4, 8
 
-WA_CUTS = (0, 4, 8, 10, 12)
+WA_CUTS = (0, 4, 6, 8, 10, 12)
+GATHER_CUTS = (0, 4, 8, 12)
 BANK_CUTS = (0, 4, 8, 12)
 FINE_CUTS = (0, 4, 8, 10, 12)
 LATE_CUTS = (0, 8, 12)
 LAST_CUTS = (0, 512, 768)
 
 VECTOR_RELUS = (5, 7, 9, 11)
-SCALAR_TURNS = (0, 1, 2, 3, 4, 5)
+SCALAR_TURNS = (0, 1, 2, 3, 5)
 
-H_BANKS = 6
-AHEAD = 2
-TURN_BANK = (6, 7, 6, 7, 6, 7)
-GATE_BANKS = ((4, 5), (6, 7))
-Y_BANKS = ((0, 1, 2, 3), (4, 5, 6), (7, 0, 1), (2, 3, 4))
+H_BANK = (0, 1, 2, 3, 6, 7, 0, 1, 2, 3, 4, 5)
+TURN_BANK = (4, 5, 0, 2, 4, 1)
+GATE_BANKS = ((6, 7), (4, 5))
+Y_BANKS = ((6, 7, 3, 0), (2, 5, 4), (1, 6, 7), (3, 0, 2))
 
 
 def spans(cuts):
@@ -98,19 +98,19 @@ def tile_moe_elr_relu_kernel(
         def load_gate(r):
             nc.sync.dma_start(out=gate_cols[:, r, :, :HALF], in_=gate[r, 0, :].rearrange("(h p c) -> p h c", h=2, c=HALF))
 
-        nc.gpsimd.memset(xs[:].bitcast(I32), 0)
+        nc.vector.memset(xs[:].bitcast(I32), 0)
         make_identity(nc, ident_raw[:])
 
         nc.sync.dma_start(out=xw[:], in_=x_words[0].rearrange("p t d -> p (t d)").bitcast(I32))
-        nc.sync.dma_start(offs_t[:], offs)
         load_gate(0)
         x_rows = x_scales[0].rearrange("(q r) t -> r q t", r=4)
         for r in range(4):
             nc.sync.dma_start(out=xs[r:P:32, :].bitcast(I32), in_=x_rows[r].bitcast(I32))
+        nc.sync.dma_start(offs_t[:], offs)
         load_wa(*spans(WA_CUTS)[0])
         load_gate(1)
         others = [(planes, row0, scales, r) for r in range(4) for row0, scales in ((W_ROW, w_scales), (WB_ROW, wb_scales))]
-        run = [load for r in range(4) for load in ((wa_plane, WA_ROW, wa_scales, r), others[r])] + others[4:]
+        run = [(wa_plane, WA_ROW, wa_scales, r) for r in range(4)] + others
         for tile, row0, scales, r in run:
             rows = scales[:, 0].rearrange("e (q r) n -> r q e n", r=4)
             nc.sync.dma_start(out=tile[row0 + r : P : 32, :, :].bitcast(I32), in_=rows[r].bitcast(I32))
@@ -147,16 +147,16 @@ def tile_moe_elr_relu_kernel(
         hs = keep.tile([P, S], U8, name="hs", align_bytes=ALIGN)
         hg = [keep.tile([P, 2 * C * 4], BF16, name="hg%d" % q, align_bytes=ALIGN) for q in range(PAIRS)]
 
-        for q in range(PAIRS):
-            slots = slice(2 * C * q, 2 * C * (q + 1))
-            entries = offs_t[:, 2 * C // 16 * q : 2 * C // 16 * (q + 1)]
+        for e0, e1 in spans(GATHER_CUTS):
+            slots = slice(C * e0, C * e1)
+            entries = offs_t[:, C // 16 * e0 : C // 16 * e1]
             nc.vector.tensor_copy(gw[:, slots], xw[:].bitcast(U32).indirect(entries))
             nc.vector.tensor_copy(gs[:, slots], xs[:].indirect(entries))
 
         def hidden(q):
             for e in (2 * q, 2 * q + 1):
                 mine = slice(C * e, C * (e + 1))
-                hp = psum.tile([P, H], F32, name="bank%d" % (e % H_BANKS))
+                hp = psum.tile([P, H], F32, name="bank%d" % H_BANK[e])
                 nc.tensor.matmul_mx(
                     out=hp[:],
                     lhsT=gw[:, mine].bitcast(FP8X4),
@@ -234,14 +234,17 @@ def tile_moe_elr_relu_kernel(
                 nc.vector.tensor_tensor(res[:], first[:, t0:t1], gated[:, t0:t1], ADD)
                 nc.sync.dma_start(out=out[P * j : P * (j + 1), t0:t1], in_=res[:])
 
-        for q in range(AHEAD):
-            hidden(q)
-        for q in range(PAIRS):
-            if q + AHEAD < PAIRS:
-                hidden(q + AHEAD)
+        hidden(0)
+        hidden(1)
+        turn(0)
+        turn(1)
+        quantise(0)
+        hidden(2)
+        for q in range(2, PAIRS):
+            if q + 1 < PAIRS:
+                hidden(q + 1)
             turn(q)
-            if q > 0:
-                quantise(q - 1)
+            quantise(q - 1)
         quantise(PAIRS - 1)
         waiting = []
         for j in range(NT):

@@ -34,7 +34,7 @@ GATHER_CUTS = (0, 4, 8, 12)
 BANK_CUTS = (0, 4, 8, 12)
 FINE_CUTS = (0, 4, 8, 10, 12)
 LATE_CUTS = (0, 8, 12)
-LAST_CUTS = (0, 512, 768)
+LAST_CUTS = (0, 384, 640, 768)
 
 VECTOR_RELUS = (5, 7, 9, 11)
 SCALAR_TURNS = (0, 1, 2, 3, 5)
@@ -56,7 +56,7 @@ def tile_moe_elr_relu_kernel(
     with ExitStack() as ctx:
         lists = ctx.enter_context(tc.tile_pool(name="lists", bufs=1))
         keep = ctx.enter_context(tc.tile_pool(name="keep", bufs=1))
-        ring = ctx.enter_context(tc.tile_pool(name="ring", bufs=NT + 1))
+        ring = ctx.enter_context(tc.tile_pool(name="ring", bufs=NT + 2))
         psum = ctx.enter_context(tc.psum_pool(name="psum", bufs=1))
 
         offs_t = lists.tile([P, S // 16], U16, name="offs_t")
@@ -110,7 +110,7 @@ def tile_moe_elr_relu_kernel(
         load_wa(*spans(WA_CUTS)[0])
         load_gate(1)
         others = [(planes, row0, scales, r) for r in range(4) for row0, scales in ((W_ROW, w_scales), (WB_ROW, wb_scales))]
-        run = [(wa_plane, WA_ROW, wa_scales, r) for r in range(4)] + others
+        run = [load for r in range(4) for load in ((wa_plane, WA_ROW, wa_scales, r), others[r])] + others[4:]
         for tile, row0, scales, r in run:
             rows = scales[:, 0].rearrange("e (q r) n -> r q e n", r=4)
             nc.sync.dma_start(out=tile[row0 + r : P : 32, :, :].bitcast(I32), in_=rows[r].bitcast(I32))
@@ -124,11 +124,12 @@ def tile_moe_elr_relu_kernel(
                     load_wb(0, 1, e0, e1)
         for r, pos in enumerate((pos1, pos2)):
             nc.sync.dma_start(pos_t[r][:], pos)
-        for e0, e1 in spans(LATE_CUTS):
-            load_wb(1, 2, e0, e1)
+        for e0, e1 in spans(BANK_CUTS)[:-1]:
+            load_wb(1, 3, e0, e1)
+        load_wb(1, 2, *spans(BANK_CUTS)[-1])
         for e0, e1 in spans(LATE_CUTS):
             load_w(2, NT, e0, e1)
-            load_wb(2, 3, e0, e1)
+        load_wb(2, 3, *spans(BANK_CUTS)[-1])
         for e0, e1 in spans(LATE_CUTS):
             load_wb(3, NT, e0, e1)
 
@@ -222,17 +223,15 @@ def tile_moe_elr_relu_kernel(
             nc.vector.tensor_tensor(first[:], y[:].indirect(pos_t[0][:]), gate_t[0][:], MULT)
             return first, second
 
-        def weigh(second, cuts):
-            gated = ring.tile([P, T], F32, name="gated")
-            for t0, t1 in spans(cuts):
-                nc.vector.tensor_tensor(gated[:, t0:t1], second[:, t0:t1], gate_t[1][:, t0:t1], MULT)
+        def weigh(second, t0, t1):
+            gated = ring.tile([P, t1 - t0], F32, name="gated")
+            nc.vector.tensor_tensor(gated[:], second[:, t0:t1], gate_t[1][:, t0:t1], MULT)
             return gated
 
-        def add(j, first, gated, cuts):
-            for t0, t1 in spans(cuts):
-                res = ring.tile([P, t1 - t0], F32, name="res", align_bytes=ALIGN)
-                nc.vector.tensor_tensor(res[:], first[:, t0:t1], gated[:, t0:t1], ADD)
-                nc.sync.dma_start(out=out[P * j : P * (j + 1), t0:t1], in_=res[:])
+        def add(j, t0, t1, first, gated):
+            res = ring.tile([P, t1 - t0], F32, name="res", align_bytes=ALIGN)
+            nc.vector.tensor_tensor(res[:], first[:, t0:t1], gated[:], ADD)
+            nc.sync.dma_start(out=out[P * j : P * (j + 1), t0:t1], in_=res[:])
 
         hidden(0)
         hidden(1)
@@ -249,8 +248,13 @@ def tile_moe_elr_relu_kernel(
         waiting = []
         for j in range(NT):
             first, second = fetch(products(j))
-            for args in waiting:
-                add(*args)
-            cuts = LAST_CUTS if j == NT - 1 else (0, T)
-            waiting = [(j, first, weigh(second, cuts), cuts)]
+            for n, (t0, t1) in enumerate(spans(LAST_CUTS if j == NT - 1 else (0, T))):
+                if n == 0:
+                    for args in waiting:
+                        add(*args)
+                    waiting = []
+                gated = weigh(second, t0, t1)
+                for args in waiting:
+                    add(*args)
+                waiting = [(j, t0, t1, first, gated)]
         add(*waiting[0])

@@ -33,7 +33,7 @@ WA_CUTS = (0, 4, 6, 8, 10, 12)
 GATHER_CUTS = (0, 4, 8, 12)
 BANK_CUTS = (0, 4, 8, 12)
 FINE_CUTS = (0, 4, 8, 10, 12)
-LATE_CUTS = (0, 8, 12)
+WB_FIRST = ((2, 0), (2, 4))
 LAST_CUTS = (0, 384, 640, 768)
 
 VECTOR_RELUS = (5, 7, 9, 11)
@@ -127,10 +127,10 @@ def tile_moe_elr_relu_kernel(
         for e0, e1 in spans(BANK_CUTS)[:-1]:
             load_wb(1, 3, e0, e1)
         load_wb(1, 2, *spans(BANK_CUTS)[-1])
-        for e0, e1 in spans(LATE_CUTS):
+        for e0, e1 in spans(BANK_CUTS):
             load_w(2, NT, e0, e1)
         load_wb(2, 3, *spans(BANK_CUTS)[-1])
-        for e0, e1 in spans(LATE_CUTS):
+        for e0, e1 in spans(BANK_CUTS):
             load_wb(3, NT, e0, e1)
 
         for r in range(2):
@@ -198,7 +198,8 @@ def tile_moe_elr_relu_kernel(
             adapter = (wb_of, FP8X4, WB_ROW, hq, hs)
             for bank, (e0, e1) in zip(Y_BANKS[j], spans(FINE_CUTS if j == 0 else BANK_CUTS)):
                 yp = psum.tile([P, (e1 - e0) * C], F32, name="bank%d" % bank)
-                for n, (weights, dtype, row0, words, scales) in enumerate((frozen, adapter)):
+                order = (adapter, frozen) if (j, e0) in WB_FIRST else (frozen, adapter)
+                for n, (weights, dtype, row0, words, scales) in enumerate(order):
                     for e in range(e0, e1):
                         mine = slice(C * e, C * (e + 1))
                         nc.tensor.matmul_mx(

@@ -22,27 +22,28 @@ ADD = mybir.AluOpType.add
 
 NT = N // P
 PAIRS = E // 2
-TB = T // P
-HALF = TB // 2
+GATE_RUN = T // (2 * P)
 
 ALIGN = 256
 
 W_ROW, WA_ROW, WB_ROW = 0, 4, 8
 
-WA_CUTS = (0, 4, 6, 8, 10, 12)
+WA_CUTS = (0, 3, 6, 8, 12)
 GATHER_CUTS = (0, 4, 8, 12)
 BANK_CUTS = (0, 4, 8, 12)
 FINE_CUTS = (0, 4, 8, 10, 12)
 WB_FIRST = ((2, 0), (2, 4))
 LAST_CUTS = (0, 384, 640, 768)
+HALVES = (0, T // 2, T)
+LAST_FUSED = 512
 
-VECTOR_RELUS = (5, 7, 9, 11)
+VECTOR_RELUS = (4, 5, 7, 9, 11)
 SCALAR_TURNS = (0, 1, 2, 3, 5)
 
 H_BANK = (0, 1, 2, 3, 6, 7, 0, 1, 2, 3, 4, 5)
-TURN_BANK = (4, 5, 0, 2, 4, 1)
+TURN_BANK = (4, 0, 6, 2, 7, 1)
 GATE_BANKS = ((6, 7), (4, 5))
-Y_BANKS = ((6, 7, 3, 0), (2, 5, 4), (1, 6, 7), (3, 0, 2))
+Y_BANKS = ((0, 6, 3, 4), (5, 2, 7), (1, 0, 6), (3, 4, 5))
 
 
 def spans(cuts):
@@ -56,7 +57,7 @@ def tile_moe_elr_relu_kernel(
     with ExitStack() as ctx:
         lists = ctx.enter_context(tc.tile_pool(name="lists", bufs=1))
         keep = ctx.enter_context(tc.tile_pool(name="keep", bufs=1))
-        ring = ctx.enter_context(tc.tile_pool(name="ring", bufs=NT + 2))
+        ring = ctx.enter_context(tc.tile_pool(name="ring", bufs=NT))
         psum = ctx.enter_context(tc.psum_pool(name="psum", bufs=1))
 
         offs_t = lists.tile([P, S // 16], U16, name="offs_t")
@@ -64,10 +65,10 @@ def tile_moe_elr_relu_kernel(
 
         xw = keep.tile([P, T], I32, name="xw", align_bytes=ALIGN)
         xs = keep.tile([P, T], U8, name="xs", align_bytes=ALIGN)
-        planes = keep.tile([P, E, N], U8, name="planes", align_bytes=ALIGN)
+        planes = [keep.tile([P, E, N // 2], U8, name="planes%d" % h, align_bytes=ALIGN) for h in range(2)]
         wa_plane = keep.tile([P, E, H], U8, name="wa_plane", align_bytes=ALIGN)
         gate_cols = keep.tile([P, 2, 2, 8], F32, name="gate_cols")
-        gate_t = [keep.tile([P, T], F32, name="gate_t%d" % r) for r in range(2)]
+        gate_t = keep.tile([P, 2 * T], F32, name="gate_t")
         ident_raw = keep.tile([P, P], F32, name="ident_raw")
         ident = keep.tile([P, P], F32, name="ident")
         wa_of, w_of, wb_of = {}, {}, {}
@@ -95,8 +96,18 @@ def tile_moe_elr_relu_kernel(
             for j in range(j0, j1):
                 w_of.update({(j, e): words[:, e - e0, 2 * P * (j - j0) : 2 * P * (j - j0 + 1)] for e in range(e0, e1)})
 
+        def load_rows(tile, row0, scales, r):
+            rows = scales[:, 0].rearrange("e (q r) n -> r q e n", r=4)
+            nc.sync.dma_start(out=tile[row0 + r : P : 32, :, :].bitcast(I32), in_=rows[r].bitcast(I32))
+
+        def half_rows(h):
+            cols = slice(N // 2 * h, N // 2 * (h + 1))
+            both = ((W_ROW, w_scales[:, :, :, cols]), (WB_ROW, wb_scales[:, :, :, cols]))
+            return [(planes[h], row0, scales, r) for r in range(4) for row0, scales in both]
+
         def load_gate(r):
-            nc.sync.dma_start(out=gate_cols[:, r, :, :HALF], in_=gate[r, 0, :].rearrange("(h p c) -> p h c", h=2, c=HALF))
+            row = gate[r, 0, :].rearrange("(h p c) -> p h c", h=2, c=GATE_RUN)
+            nc.sync.dma_start(out=gate_cols[:, r, :, :GATE_RUN], in_=row)
 
         nc.vector.memset(xs[:].bitcast(I32), 0)
         make_identity(nc, ident_raw[:])
@@ -109,11 +120,12 @@ def tile_moe_elr_relu_kernel(
         nc.sync.dma_start(offs_t[:], offs)
         load_wa(*spans(WA_CUTS)[0])
         load_gate(1)
-        others = [(planes, row0, scales, r) for r in range(4) for row0, scales in ((W_ROW, w_scales), (WB_ROW, wb_scales))]
-        run = [load for r in range(4) for load in ((wa_plane, WA_ROW, wa_scales, r), others[r])] + others[4:]
-        for tile, row0, scales, r in run:
-            rows = scales[:, 0].rearrange("e (q r) n -> r q e n", r=4)
-            nc.sync.dma_start(out=tile[row0 + r : P : 32, :, :].bitcast(I32), in_=rows[r].bitcast(I32))
+        others = [half_rows(0), half_rows(1)]
+        for r in range(4):
+            load_rows(wa_plane, WA_ROW, wa_scales, r)
+            load_rows(*others[0][r])
+        for load in others[0][4:]:
+            load_rows(*load)
         nc.scalar.activation(ident[:], ident_raw[:], ACT.Relu)
         for e0, e1 in spans(WA_CUTS)[1:]:
             load_wa(e0, e1)
@@ -127,6 +139,8 @@ def tile_moe_elr_relu_kernel(
         for e0, e1 in spans(BANK_CUTS)[:-1]:
             load_wb(1, 3, e0, e1)
         load_wb(1, 2, *spans(BANK_CUTS)[-1])
+        for load in others[1]:
+            load_rows(*load)
         for e0, e1 in spans(BANK_CUTS):
             load_w(2, NT, e0, e1)
         load_wb(2, 3, *spans(BANK_CUTS)[-1])
@@ -135,11 +149,11 @@ def tile_moe_elr_relu_kernel(
 
         for r in range(2):
             for h, bank in enumerate(GATE_BANKS[r]):
-                spread = psum.tile([P, HALF, P], F32, name="bank%d" % bank)
-                for c in range(HALF):
+                spread = psum.tile([P, GATE_RUN, P], F32, name="bank%d" % bank)
+                for c in range(GATE_RUN):
                     nc.tensor.transpose(spread[:, c, :], gate_cols[:, r, h, c : c + 1].to_broadcast([P, P]), ident[:])
-                half = gate_t[r][:, T // 2 * h : T // 2 * (h + 1)]
-                nc.scalar.copy(half.rearrange("p (n c) -> p n c", c=HALF), spread[:].rearrange("p c n -> p n c"))
+                half = gate_t[:, T * r + T // 2 * h : T * r + T // 2 * (h + 1)]
+                nc.scalar.copy(half.rearrange("p (n c) -> p n c", c=GATE_RUN), spread[:].rearrange("p c n -> p n c"))
 
         gw = keep.tile([P, S], U32, name="gw", align_bytes=ALIGN)
         gs = keep.tile([P, S], U8, name="gs", align_bytes=ALIGN)
@@ -193,7 +207,7 @@ def tile_moe_elr_relu_kernel(
 
         def products(j):
             y = keep.tile([P, S], F32, name="y%d" % j)
-            cols = slice(P * j, P * (j + 1))
+            cols = slice(P * (j % 2), P * (j % 2 + 1))
             frozen = (w_of, FP4X4, W_ROW, gw, gs)
             adapter = (wb_of, FP8X4, WB_ROW, hq, hs)
             for bank, (e0, e1) in zip(Y_BANKS[j], spans(FINE_CUTS if j == 0 else BANK_CUTS)):
@@ -205,7 +219,7 @@ def tile_moe_elr_relu_kernel(
                         nc.tensor.matmul_mx(
                             out=yp[:, C * (e - e0) : C * (e - e0 + 1)],
                             lhsT=weights[j, e].bitcast(dtype),
-                            lhsT_scale=planes[row0:P, e, cols],
+                            lhsT_scale=planes[j // 2][row0:P, e, cols],
                             rhs=words[:, mine].bitcast(FP8X4),
                             rhs_scale=scales[:, mine],
                             start=n == 0 and e == e0,
@@ -217,45 +231,51 @@ def tile_moe_elr_relu_kernel(
                     nc.scalar.copy(y[:, C * e0 : C * e1], yp[:])
             return y
 
-        def fetch(y):
-            second = ring.tile([P, T], F32, name="second")
-            nc.scalar.activation(second[:], y[:].indirect(pos_t[1][:]), ACT.Copy)
-            first = ring.tile([P, T], F32, name="first")
-            nc.vector.tensor_tensor(first[:], y[:].indirect(pos_t[0][:]), gate_t[0][:], MULT)
-            return first, second
+        def fetch(y, fused, cuts):
+            plain = ring.tile([P, 2 * T], F32, name="plain")
+            if fused < T:
+                nc.scalar.activation(plain[:, fused:T], y[:].indirect(pos_t[0][:, fused // 16 :]), ACT.Copy)
+            for t0, t1 in spans(cuts):
+                picked = y[:].indirect(pos_t[1][:, t0 // 16 : t1 // 16])
+                nc.scalar.activation(plain[:, T + t0 : T + t1], picked, ACT.Copy)
+            gated = ring.tile([P, 2 * T], F32, name="gated")
+            picked = y[:].indirect(pos_t[0][:, : fused // 16])
+            nc.vector.tensor_tensor(gated[:, :fused], picked, gate_t[:, :fused], MULT)
+            return gated, plain
 
-        def weigh(second, t0, t1):
-            gated = ring.tile([P, t1 - t0], F32, name="gated")
-            nc.vector.tensor_tensor(gated[:], second[:, t0:t1], gate_t[1][:, t0:t1], MULT)
-            return gated
+        def weigh(gated, plain, fused, t0, t1):
+            cols = slice(T + t0 if t0 else fused, T + t1)
+            nc.vector.tensor_tensor(gated[:, cols], plain[:, cols], gate_t[:, cols], MULT)
 
-        def add(j, t0, t1, first, gated):
-            res = ring.tile([P, t1 - t0], F32, name="res", align_bytes=ALIGN)
-            nc.vector.tensor_tensor(res[:], first[:, t0:t1], gated[:], ADD)
+        def add(j, t0, t1, gated):
+            res = keep.tile([P, t1 - t0], F32, name="res%d_%d" % (j, t0), align_bytes=ALIGN)
+            nc.vector.tensor_tensor(res[:], gated[:, t0:t1], gated[:, T + t0 : T + t1], ADD)
             nc.sync.dma_start(out=out[P * j : P * (j + 1), t0:t1], in_=res[:])
 
         hidden(0)
         hidden(1)
         turn(0)
+        hidden(2)
+        hidden(3)
         turn(1)
         quantise(0)
-        hidden(2)
-        for q in range(2, PAIRS):
-            if q + 1 < PAIRS:
-                hidden(q + 1)
+        turn(2)
+        quantise(1)
+        hidden(4)
+        hidden(5)
+        for q in range(3, PAIRS):
             turn(q)
             quantise(q - 1)
         quantise(PAIRS - 1)
+
         waiting = []
         for j in range(NT):
-            first, second = fetch(products(j))
-            for n, (t0, t1) in enumerate(spans(LAST_CUTS if j == NT - 1 else (0, T))):
-                if n == 0:
-                    for args in waiting:
-                        add(*args)
-                    waiting = []
-                gated = weigh(second, t0, t1)
+            last = j == NT - 1
+            fused = LAST_FUSED if last else T
+            gated, plain = fetch(products(j), fused, LAST_CUTS if last else (0, T))
+            for t0, t1 in spans(LAST_CUTS if last else HALVES):
+                weigh(gated, plain, fused, t0, t1)
                 for args in waiting:
                     add(*args)
-                waiting = [(j, t0, t1, first, gated)]
+                waiting = [(j, t0, t1, gated)]
         add(*waiting[0])

@@ -22,7 +22,7 @@ ADD = mybir.AluOpType.add
 
 NT = N // P
 PAIRS = E // 2
-GATE_RUN = T // (2 * P)
+GATE_RUN = 2 * T // P
 
 ALIGN = 256
 
@@ -42,7 +42,7 @@ SCALAR_TURNS = (0, 1, 2, 3, 5)
 
 H_BANK = (0, 1, 2, 3, 6, 7, 0, 1, 2, 3, 4, 5)
 TURN_BANK = (4, 0, 6, 2, 7, 1)
-GATE_BANKS = ((6, 7), (4, 5))
+GATE_BANKS = (6, 7, 5)
 Y_BANKS = ((0, 6, 3, 4), (5, 2, 7), (1, 0, 6), (3, 4, 5))
 
 
@@ -65,9 +65,9 @@ def tile_moe_elr_relu_kernel(
 
         xw = keep.tile([P, T], I32, name="xw", align_bytes=ALIGN)
         xs = keep.tile([P, T], U8, name="xs", align_bytes=ALIGN)
-        planes = [keep.tile([P, E, N // 2], U8, name="planes%d" % h, align_bytes=ALIGN) for h in range(2)]
+        planes = keep.tile([P, E, N], U8, name="planes", align_bytes=ALIGN)
         wa_plane = keep.tile([P, E, H], U8, name="wa_plane", align_bytes=ALIGN)
-        gate_cols = keep.tile([P, 2, 2, 8], F32, name="gate_cols")
+        gate_cols = keep.tile([P, GATE_RUN], F32, name="gate_cols")
         gate_t = keep.tile([P, 2 * T], F32, name="gate_t")
         ident_raw = keep.tile([P, P], F32, name="ident_raw")
         ident = keep.tile([P, P], F32, name="ident")
@@ -100,31 +100,23 @@ def tile_moe_elr_relu_kernel(
             rows = scales[:, 0].rearrange("e (q r) n -> r q e n", r=4)
             nc.sync.dma_start(out=tile[row0 + r : P : 32, :, :].bitcast(I32), in_=rows[r].bitcast(I32))
 
-        def half_rows(h):
-            cols = slice(N // 2 * h, N // 2 * (h + 1))
-            both = ((W_ROW, w_scales[:, :, :, cols]), (WB_ROW, wb_scales[:, :, :, cols]))
-            return [(planes[h], row0, scales, r) for r in range(4) for row0, scales in both]
-
-        def load_gate(r):
-            row = gate[r, 0, :].rearrange("(h p c) -> p h c", h=2, c=GATE_RUN)
-            nc.sync.dma_start(out=gate_cols[:, r, :, :GATE_RUN], in_=row)
 
         nc.vector.memset(xs[:].bitcast(I32), 0)
         make_identity(nc, ident_raw[:])
 
         nc.sync.dma_start(out=xw[:], in_=x_words[0].rearrange("p t d -> p (t d)").bitcast(I32))
-        load_gate(0)
+        both = gate.rearrange("r p t -> (r p t)")[(P - 1) * T : (P + 1) * T]
+        nc.sync.dma_start(out=gate_cols[:], in_=both.rearrange("(p c) -> p c", c=GATE_RUN))
         x_rows = x_scales[0].rearrange("(q r) t -> r q t", r=4)
         for r in range(4):
             nc.sync.dma_start(out=xs[r:P:32, :].bitcast(I32), in_=x_rows[r].bitcast(I32))
         nc.sync.dma_start(offs_t[:], offs)
         load_wa(*spans(WA_CUTS)[0])
-        load_gate(1)
-        others = [half_rows(0), half_rows(1)]
+        others = [(planes, *plane, r) for r in range(4) for plane in ((W_ROW, w_scales), (WB_ROW, wb_scales))]
         for r in range(4):
             load_rows(wa_plane, WA_ROW, wa_scales, r)
-            load_rows(*others[0][r])
-        for load in others[0][4:]:
+            load_rows(*others[r])
+        for load in others[4:]:
             load_rows(*load)
         nc.scalar.activation(ident[:], ident_raw[:], ACT.Relu)
         for e0, e1 in spans(WA_CUTS)[1:]:
@@ -139,21 +131,18 @@ def tile_moe_elr_relu_kernel(
         for e0, e1 in spans(BANK_CUTS)[:-1]:
             load_wb(1, 3, e0, e1)
         load_wb(1, 2, *spans(BANK_CUTS)[-1])
-        for load in others[1]:
-            load_rows(*load)
         for e0, e1 in spans(BANK_CUTS):
             load_w(2, NT, e0, e1)
         load_wb(2, 3, *spans(BANK_CUTS)[-1])
         for e0, e1 in spans(BANK_CUTS):
             load_wb(3, NT, e0, e1)
 
-        for r in range(2):
-            for h, bank in enumerate(GATE_BANKS[r]):
-                spread = psum.tile([P, GATE_RUN, P], F32, name="bank%d" % bank)
-                for c in range(GATE_RUN):
-                    nc.tensor.transpose(spread[:, c, :], gate_cols[:, r, h, c : c + 1].to_broadcast([P, P]), ident[:])
-                half = gate_t[:, T * r + T // 2 * h : T * r + T // 2 * (h + 1)]
-                nc.scalar.copy(half.rearrange("p (n c) -> p n c", c=GATE_RUN), spread[:].rearrange("p c n -> p n c"))
+        for b, bank in enumerate(GATE_BANKS):
+            spread = psum.tile([P, 4, P], F32, name="bank%d" % bank)
+            for c in range(4):
+                nc.tensor.transpose(spread[:, c, :], gate_cols[:, 4 * b + c : 4 * b + c + 1].to_broadcast([P, P]), ident[:])
+            dst = gate_t[:].rearrange("p (n c) -> p n c", c=GATE_RUN)[:, :, 4 * b : 4 * (b + 1)]
+            nc.scalar.copy(dst, spread[:].rearrange("p c n -> p n c"))
 
         gw = keep.tile([P, S], U32, name="gw", align_bytes=ALIGN)
         gs = keep.tile([P, S], U8, name="gs", align_bytes=ALIGN)
@@ -207,7 +196,7 @@ def tile_moe_elr_relu_kernel(
 
         def products(j):
             y = keep.tile([P, S], F32, name="y%d" % j)
-            cols = slice(P * (j % 2), P * (j % 2 + 1))
+            cols = slice(P * j, P * (j + 1))
             frozen = (w_of, FP4X4, W_ROW, gw, gs)
             adapter = (wb_of, FP8X4, WB_ROW, hq, hs)
             for bank, (e0, e1) in zip(Y_BANKS[j], spans(FINE_CUTS if j == 0 else BANK_CUTS)):
@@ -219,7 +208,7 @@ def tile_moe_elr_relu_kernel(
                         nc.tensor.matmul_mx(
                             out=yp[:, C * (e - e0) : C * (e - e0 + 1)],
                             lhsT=weights[j, e].bitcast(dtype),
-                            lhsT_scale=planes[j // 2][row0:P, e, cols],
+                            lhsT_scale=planes[row0:P, e, cols],
                             rhs=words[:, mine].bitcast(FP8X4),
                             rhs_scale=scales[:, mine],
                             start=n == 0 and e == e0,

from contextlib import ExitStack

import concourse.mybir as mybir
from concourse.masks import make_identity

K, T, E, C, H, N = 512, 768, 12, 128, 512, 512
S = E * C
P = 128
FLOPS = 2 * 3 * S * K * N

F32 = mybir.dt.float32
BF16 = mybir.dt.bfloat16
I32 = mybir.dt.int32
U32 = mybir.dt.uint32
U16 = mybir.dt.uint16
U8 = mybir.dt.uint8
FP8X4 = mybir.dt.float8_e4m3fn_x4
FP4X4 = mybir.dt.float4_e2m1fn_x4
ACT = mybir.ActivationFunctionType
MULT = mybir.AluOpType.mult
ADD = mybir.AluOpType.add

NT = N // P
PAIRS = E // 2
GATE_RUN = 2 * T // P

ALIGN = 256

W_ROW, WA_ROW, WB_ROW = 0, 4, 8

WA_CUTS = (0, 3, 6, 8, 12)
GATHER_CUTS = (0, 4, 8, 12)
BANK_CUTS = (0, 4, 8, 12)
FINE_CUTS = (0, 4, 8, 10, 12)
WB_FIRST = ((2, 0), (2, 4))
LAST_CUTS = (0, 384, 640, 768)
HALVES = (0, T // 2, T)
LAST_FUSED = 512

VECTOR_RELUS = (4, 5, 7, 9, 11)
SCALAR_TURNS = (0, 1, 2, 3, 5)

H_BANK = (0, 1, 2, 3, 6, 7, 0, 1, 2, 3, 4, 5)
TURN_BANK = (4, 0, 6, 2, 7, 1)
GATE_BANKS = (6, 7, 5)
Y_BANKS = ((0, 6, 3, 4), (5, 2, 7), (1, 0, 6), (3, 4, 5))


def spans(cuts):
    return list(zip(cuts[:-1], cuts[1:]))


def tile_moe_elr_relu_kernel(
    tc, x_words, x_scales, w_words, w_scales, wa_words, wa_scales, wb_words, wb_scales, gate, offs, pos1, pos2, out
):
    nc = tc.nc
    with ExitStack() as ctx:
        lists = ctx.enter_context(tc.tile_pool(name="lists", bufs=1))
        keep = ctx.enter_context(tc.tile_pool(name="keep", bufs=1))
        ring = ctx.enter_context(tc.tile_pool(name="ring", bufs=NT))
        psum = ctx.enter_context(tc.psum_pool(name="psum", bufs=1))

        offs_t = lists.tile([P, S // 16], U16, name="offs_t")
        pos_t = [lists.tile([P, T // 16], U16, name="pos%d_t" % r) for r in (1, 2)]

        xw = keep.tile([P, T], I32, name="xw", align_bytes=ALIGN)
        xs = keep.tile([P, T], U8, name="xs", align_bytes=ALIGN)
        planes = keep.tile([P, E, N], U8, name="planes", align_bytes=ALIGN)
        wa_plane = keep.tile([P, E, H], U8, name="wa_plane", align_bytes=ALIGN)
        gate_cols = keep.tile([P, GATE_RUN], F32, name="gate_cols")
        gate_t = keep.tile([P, 2 * T], F32, name="gate_t")
        ident_raw = keep.tile([P, P], F32, name="ident_raw")
        ident = keep.tile([P, P], F32, name="ident")
        wa_of, w_of, wb_of = {}, {}, {}

        def load_wa(e0, e1):
            words = keep.tile([P, e1 - e0, H], I32, name="wa_t%d" % e0, align_bytes=ALIGN)
            nc.sync.dma_start(out=words[:], in_=wa_words[e0:e1, 0].rearrange("e p i d -> p e (i d)").bitcast(I32))
            wa_of.update({e: words[:, e - e0, :] for e in range(e0, e1)})

        def load_wb(j0, j1, e0, e1):
            words = keep.tile([P, e1 - e0, P * (j1 - j0)], I32, name="wb_t%d_%d" % (j0, e0), align_bytes=ALIGN)
            nc.sync.dma_start(
                out=words[:],
                in_=wb_words[e0:e1, 0, :, P * j0 : P * j1, :].rearrange("e p n d -> p e (n d)").bitcast(I32),
            )
            for j in range(j0, j1):
                wb_of.update({(j, e): words[:, e - e0, P * (j - j0) : P * (j - j0 + 1)] for e in range(e0, e1)})

        def load_w(j0, j1, e0, e1):
            words = keep.tile([P, e1 - e0, 2 * P * (j1 - j0)], U8, name="w_t%d_%d" % (j0, e0), align_bytes=ALIGN)
            nc.sync.dma_start(
                out=words[:].bitcast(I32),
                in_=w_words[e0:e1, 0, :, 2 * P * j0 : 2 * P * j1].rearrange("e p b -> p e b").bitcast(I32),
            )
            for j in range(j0, j1):
                w_of.update({(j, e): words[:, e - e0, 2 * P * (j - j0) : 2 * P * (j - j0 + 1)] for e in range(e0, e1)})

        def load_rows(tile, row0, scales, r):
            rows = scales[:, 0].rearrange("e (q r) n -> r q e n", r=4)
            nc.sync.dma_start(out=tile[row0 + r : P : 32, :, :].bitcast(I32), in_=rows[r].bitcast(I32))


        nc.vector.memset(xs[:].bitcast(I32), 0)
        make_identity(nc, ident_raw[:])

        nc.sync.dma_start(out=xw[:], in_=x_words[0].rearrange("p t d -> p (t d)").bitcast(I32))
        both = gate.rearrange("r p t -> (r p t)")[(P - 1) * T : (P + 1) * T]
        nc.sync.dma_start(out=gate_cols[:], in_=both.rearrange("(p c) -> p c", c=GATE_RUN))
        x_rows = x_scales[0].rearrange("(q r) t -> r q t", r=4)
        for r in range(4):
            nc.sync.dma_start(out=xs[r:P:32, :].bitcast(I32), in_=x_rows[r].bitcast(I32))
        nc.sync.dma_start(offs_t[:], offs)
        load_wa(*spans(WA_CUTS)[0])
        others = [(planes, *plane, r) for r in range(4) for plane in ((W_ROW, w_scales), (WB_ROW, wb_scales))]
        for r in range(4):
            load_rows(wa_plane, WA_ROW, wa_scales, r)
            load_rows(*others[r])
        for load in others[4:]:
            load_rows(*load)
        nc.scalar.activation(ident[:], ident_raw[:], ACT.Relu)
        for e0, e1 in spans(WA_CUTS)[1:]:
            load_wa(e0, e1)
        for g0, g1 in spans(BANK_CUTS):
            load_w(0, 2, g0, g1)
            for e0, e1 in spans(FINE_CUTS):
                if g0 <= e0 < g1:
                    load_wb(0, 1, e0, e1)
        for r, pos in enumerate((pos1, pos2)):
            nc.sync.dma_start(pos_t[r][:], pos)
        for e0, e1 in spans(BANK_CUTS)[:-1]:
            load_wb(1, 3, e0, e1)
        load_wb(1, 2, *spans(BANK_CUTS)[-1])
        for e0, e1 in spans(BANK_CUTS):
            load_w(2, NT, e0, e1)
        load_wb(2, 3, *spans(BANK_CUTS)[-1])
        for e0, e1 in spans(BANK_CUTS):
            load_wb(3, NT, e0, e1)

        for b, bank in enumerate(GATE_BANKS):
            spread = psum.tile([P, 4, P], F32, name="bank%d" % bank)
            for c in range(4):
                nc.tensor.transpose(spread[:, c, :], gate_cols[:, 4 * b + c : 4 * b + c + 1].to_broadcast([P, P]), ident[:])
            dst = gate_t[:].rearrange("p (n c) -> p n c", c=GATE_RUN)[:, :, 4 * b : 4 * (b + 1)]
            nc.scalar.copy(dst, spread[:].rearrange("p c n -> p n c"))

        gw = keep.tile([P, S], U32, name="gw", align_bytes=ALIGN)
        gs = keep.tile([P, S], U8, name="gs", align_bytes=ALIGN)
        hb = [keep.tile([P, H], BF16, name="hb%d" % e, align_bytes=ALIGN) for e in range(E)]
        hq = keep.tile([P, S], U32, name="hq", align_bytes=ALIGN)
        hs = keep.tile([P, S], U8, name="hs", align_bytes=ALIGN)
        hg = [keep.tile([P, 2 * C * 4], BF16, name="hg%d" % q, align_bytes=ALIGN) for q in range(PAIRS)]

        for e0, e1 in spans(GATHER_CUTS):
            slots = slice(C * e0, C * e1)
            entries = offs_t[:, C // 16 * e0 : C // 16 * e1]
            nc.vector.tensor_copy(gw[:, slots], xw[:].bitcast(U32).indirect(entries))
            nc.vector.tensor_copy(gs[:, slots], xs[:].indirect(entries))

        def hidden(q):
            for e in (2 * q, 2 * q + 1):
                mine = slice(C * e, C * (e + 1))
                hp = psum.tile([P, H], F32, name="bank%d" % H_BANK[e])
                nc.tensor.matmul_mx(
                    out=hp[:],
                    lhsT=gw[:, mine].bitcast(FP8X4),
                    lhsT_scale=gs[:, mine],
                    rhs=wa_of[e].bitcast(FP8X4),
                    rhs_scale=wa_plane[WA_ROW:P, e, :],
                    start=True,
                    stop=True,
                )
                dst = hb[e][:].rearrange("s (u p d) -> s u p d", u=2, d=2)
                src = hp[:].rearrange("s (p u d) -> s u p d", u=2, d=2)
                if e in VECTOR_RELUS:
                    nc.vector.tensor_scalar_max(dst, src, 0.0)
                else:
                    nc.scalar.activation(dst, src, ACT.Relu)

        def turn(q):
            tp = psum.tile([P, 2, 2, C], F32, name="bank%d" % TURN_BANK[q])
            for a in range(2):
                words = hb[2 * q + a][:].bitcast(F32)
                for u in range(2):
                    nc.tensor.transpose(tp[:, a, u, :], words[:, P * u : P * (u + 1)], ident[:])
            dst = hg[q][:].bitcast(F32).rearrange("p (a s u) -> p a s u", a=2, u=2)
            src = tp[:].rearrange("p a u s -> p a s u")
            if q in SCALAR_TURNS:
                nc.scalar.copy(dst, src)
            else:
                nc.vector.tensor_copy(dst, src)

        def quantise(q):
            slots = slice(2 * C * q, 2 * C * (q + 1))
            nc.vector.quantize_mx(out=hq[:, slots].bitcast(FP8X4), scales=hs[:, slots], in_=hg[q][:])

        def products(j):
            y = keep.tile([P, S], F32, name="y%d" % j)
            cols = slice(P * j, P * (j + 1))
            frozen = (w_of, FP4X4, W_ROW, gw, gs)
            adapter = (wb_of, FP8X4, WB_ROW, hq, hs)
            for bank, (e0, e1) in zip(Y_BANKS[j], spans(FINE_CUTS if j == 0 else BANK_CUTS)):
                yp = psum.tile([P, (e1 - e0) * C], F32, name="bank%d" % bank)
                order = (adapter, frozen) if (j, e0) in WB_FIRST else (frozen, adapter)
                for n, (weights, dtype, row0, words, scales) in enumerate(order):
                    for e in range(e0, e1):
                        mine = slice(C * e, C * (e + 1))
                        nc.tensor.matmul_mx(
                            out=yp[:, C * (e - e0) : C * (e - e0 + 1)],
                            lhsT=weights[j, e].bitcast(dtype),
                            lhsT_scale=planes[row0:P, e, cols],
                            rhs=words[:, mine].bitcast(FP8X4),
                            rhs_scale=scales[:, mine],
                            start=n == 0 and e == e0,
                            stop=n == 1 and e == e1 - 1,
                        )
                if j == 0 and e1 == E:
                    nc.vector.tensor_copy(y[:, C * e0 : C * e1], yp[:])
                else:
                    nc.scalar.copy(y[:, C * e0 : C * e1], yp[:])
            return y

        def fetch(y, fused, cuts):
            plain = ring.tile([P, 2 * T], F32, name="plain")
            if fused < T:
                nc.scalar.activation(plain[:, fused:T], y[:].indirect(pos_t[0][:, fused // 16 :]), ACT.Copy)
            for t0, t1 in spans(cuts):
                picked = y[:].indirect(pos_t[1][:, t0 // 16 : t1 // 16])
                nc.scalar.activation(plain[:, T + t0 : T + t1], picked, ACT.Copy)
            gated = ring.tile([P, 2 * T], F32, name="gated")
            picked = y[:].indirect(pos_t[0][:, : fused // 16])
            nc.vector.tensor_tensor(gated[:, :fused], picked, gate_t[:, :fused], MULT)
            return gated, plain

        def weigh(gated, plain, fused, t0, t1):
            cols = slice(T + t0 if t0 else fused, T + t1)
            nc.vector.tensor_tensor(gated[:, cols], plain[:, cols], gate_t[:, cols], MULT)

        def add(j, t0, t1, gated):
            res = keep.tile([P, t1 - t0], F32, name="res%d_%d" % (j, t0), align_bytes=ALIGN)
            nc.vector.tensor_tensor(res[:], gated[:, t0:t1], gated[:, T + t0 : T + t1], ADD)
            nc.sync.dma_start(out=out[P * j : P * (j + 1), t0:t1], in_=res[:])

        hidden(0)
        hidden(1)
        turn(0)
        hidden(2)
        hidden(3)
        turn(1)
        quantise(0)
        turn(2)
        quantise(1)
        hidden(4)
        hidden(5)
        for q in range(3, PAIRS):
            turn(q)
            quantise(q - 1)
        quantise(PAIRS - 1)

        waiting = []
        for j in range(NT):
            last = j == NT - 1
            fused = LAST_FUSED if last else T
            gated, plain = fetch(products(j), fused, LAST_CUTS if last else (0, T))
            for t0, t1 in spans(LAST_CUTS if last else HALVES):
                weigh(gated, plain, fused, t0, t1)
                for args in waiting:
                    add(*args)
                waiting = [(j, t0, t1, gated)]
        add(*waiting[0])
